import numpy as np, ml_dtypes
CORES = [8,136,40,168]
N = 4
BF = ml_dtypes.bfloat16
def gentries(a):
    return np.ascontiguousarray(a.reshape(8, 16, -1).transpose(0, 2, 1)).reshape(8, -1)
def gtable(e):
    e = np.asarray(e); return np.ascontiguousarray(e.reshape(8, -1, 16).transpose(0, 2, 1)).reshape(128, -1).astype(np.int32)
G, C, P, RO, YC = 64, 64, 128, 3, 32
W, LG, LC, H, M = 4096, 6, 6, 32, 16
BIG = 2 ** 24
def probes(u, k):
    return (((u * u) >> 5)[..., None] + u[..., None] * k) & (W - 1)
def base(rng):
    ring = rng.integers(0, 256, (8, 8, 64, 16)); a = rng.integers(0, 8, (N, 8, G, 1)); b = rng.integers(0, 64, (N, 8, G, 1))
    X = ring[np.arange(8)[None, :, None, None], a, (b + np.arange(C)) & 63]
    X = np.clip(X + rng.integers(-4, 5, X.shape), 0, 255)
    th = np.where(rng.random((N, 8, P)) < 0.25, rng.integers(0, 300, (N, 8, P)), rng.integers(600, 1600, (N, 8, P)))
    return X, rng.integers(1, 256, (N, 8, 16)), rng.integers(0, 2048, (N, 8, RO, P)), th
def pack(X, wt, km, th):
    X = np.ascontiguousarray(X.reshape(N, 8, G, C, 16).transpose(0, 1, 4, 2, 3)).reshape(N, 128, W)
    return {"gen0": X.astype(np.float32).astype(BF), "wt": np.ascontiguousarray(wt.reshape(N, 128, 1)).astype(np.int32),
            "km": np.stack([gtable(a.reshape(8, -1)) for a in km]), "th": np.stack([gtable(a) for a in th])}
def setup_inputs(rng):
    return pack(*base(rng))
def column(rng, w, u):
    x = rng.integers(0, 256, 16); r = (int(u) - int(np.sum(w[2:] * x[2:]))) & (W - 1); x[0] = r & 15; x[1] = r >> 4
    return x
def link(rng, Y, w, k, o, alone=False):
    c = probes(np.arange(W)[None, :], k[None, None, :])[0]
    od = np.argsort(c.reshape(-1).astype(np.int16), kind="stable"); st = np.searchsorted(c.reshape(-1)[od], np.arange(W + 1))
    for i in range(G - 1):
        if alone and i == 1: continue
        j = 2 if alone and i == 0 else i + 1
        t = C * j + int(o[i]); us = od[st[t]:st[t + 1]] // P; us = us[~np.any(c[us] == C * i + C - 1, axis=1)]
        if len(us):
            x = column(rng, w, us[int(rng.integers(0, len(us)))]); Y[i, C - 1] = x; Y[j, int(o[i])] = x
def setup_inputs_deep(rng):
    X, wt, km, th = base(rng); th = rng.integers(30, 41, th.shape); B = 8 * N; b = np.arange(B)
    X = X.reshape(B, G, C, 16); w = wt.reshape(B, 1, 16).astype(np.int32); k0 = km[:, :, 0].reshape(B, 1, P).astype(np.int32); tries = min(128, max(16, 16 * G // P))
    for i in range(G - 1):
        x = rng.integers(0, 256, (B, tries, 16), dtype=np.int32); u = (np.sum(w * x, axis=2) & (W - 1)).astype(np.int32)
        c = probes(u, k0); o = c & (C - 1); to = np.where((b % 4 == 2) & (i == 0), 2, i + 1)
        hit = ((c >> LC) == to[:, None, None]) & (o != C - 1) & ~np.any(c == C * i + C - 1, axis=2)[..., None]
        like = np.where((b % 4 == 0)[:, None, None], o, np.where((b % 4 == 2)[:, None, None], C - 1 - o, 0)) + 1
        s = np.where(hit, like, 0).reshape(B, -1); a = np.argmax(s, axis=1)
        do = (s[b, a] > 0) & ((b % 2 == 0) | (rng.random(B) < 0.9)) & ((b % 4 != 2) | (i != 1))
        bb = b[do]; aa = a[do]; xs = x[bb, aa // P]
        X[bb, i, C - 1] = xs; X[bb, to[bb], o.reshape(B, -1)[bb, aa]] = xs
    X = X.reshape(N, 8, G, C, 16)
    for g in (3, 4, 7):
        wt[:, g, 0] = 1; wt[:, g, 1] = 16
    for r in range(N): link(rng, X[r, 4], wt[r, 4], km[r, 4, 0], np.full(G, C - 2))
    k = np.arange(2048)
    for g in (3, 7):
        h = int(rng.choice(np.array([3, 5, 7, 9]))); q0 = int(np.argmin((np.arange(C) * h + 1) & (C - 1))); Y = X[:, g].copy()
        for r in range(N):
            u = h - 1 + H * int(rng.integers(0, W // H)); c = (u * u // 32 + k * u) & (W - 1)
            km[r, g, 0] = rng.choice(k[(c & (C - 1)) != C - 1], P); Y[:, r * M:(r + 1) * M, q0] = column(rng, wt[r, g], u)
        for d in range(N): link(rng, Y[d], wt[d, g], km[d, g, 1], np.full(G, C - 2) if g == 3 else 2 * rng.integers(0, C // 2, G), g == 7)
        p = (C * np.arange(G)[:, None] + h * np.arange(C)) & (W - 1)
        for r in range(N):
            kid = np.zeros((G, C, 16), np.int64)
            for d in range(N): kid[(d - r) % N::N] = Y[d, r * M:(r + 1) * M]
            X[r, g, p >> LC, p & (C - 1)] = kid
    return pack(X, wt, km, th)
def setup_inputs_edges(rng):
    X, wt, km, th = base(rng)
    th[:, 0] = 0; e = X[:, 0, :1, C - 1].copy(); X[:, 0, ::2, C - 1] = e; X[:, 0, :, ::4] = e[:, :, None]
    f = rng.integers(0, 16, (N, G, C, 1)); X[:, 1] = (np.arange(16) == f) & (rng.random((N, G, C, 1)) < 0.2); X[:, 1, :, C - 1] = 255; th[:, 1] = 4080
    k = np.arange(2048)
    for q in range(N):
        u = int(255 * np.sum(wt[q, 1])) & (W - 1); c = ((u * u >> 5) + k * u) & (W - 1)
        good = k[(c & (C - 1)) != C - 1]
        km[q, 1, 0] = rng.choice(good if len(good) else k, P)
    km[:, 2] = rng.choice(np.array([0, 1, 3, 2047]), (N, RO, P))
    X[:, 3, ::2, C - 1] = 0; X[:, 3, 0, 0] = 0
    wt[:, 4] = 255; X[:, 4] = 255 - rng.integers(0, 3, (N, G, C, 16))
    X[:, 5, :, C - 1] = rng.integers(0, 256, (N, 1, 16))
    X[:, 6] = 255 * rng.integers(0, 2, (N, G, C, 16)); th[:, 6] = 255 * rng.integers(2, 9, (N, P))
    return pack(X, wt, km, th)
def setup_inputs_far(rng):
    X, wt, km, th = base(rng); k = np.arange(2048)
    for q in range(N):
        for g in (0, 1, 2, 4, 5):
            wt[q, g, 0] |= 1; wt[q, g, 8:] = wt[q, g, :8]
            b = np.concatenate([rng.integers(110, 181, (256, 8)), rng.integers(80, 101, (256, 8))], axis=1); u = np.sum(wt[q, g] * b, axis=1) & (W - 1)
            c = probes(u[None, :], k[None, None, :])[0]
            ok = (c == W - 1) if g == 4 else (c >= 3 * W // 4) & ((c & (C - 1)) != C - 1)
            if g == 5: ok = ok & np.any(c == 0, axis=1)[:, None]
            a, m = np.nonzero(ok); s = int(rng.integers(0, len(a))); x = b[a[s]]; c = c[a[s]]; K = int(m[s]); j = int(c[K]) >> LC; o = int(c[K]) & (C - 1)
            e = rng.integers(35, 71, (G, 8)); e[G // 4:G // 2] = rng.integers(0, 35, (G // 2 - G // 4, 8))
            if g > 2: e[:] = 0
            last = x + np.concatenate([e, -e], axis=1); X[q, g, :, C - 1] = last; km[q, g, 0] = K
            if g == 1:
                km[q, 1, 0] = rng.choice(k[(c & (C - 1)) != C - 1], P); th[q, 1] = rng.integers(2048, 4081, P)
                X[q, 1, :, :C - 1, :8] = rng.integers(0, 41, (G, C - 1, 8)); X[q, 1, :, :C - 1, 8:] = rng.integers(215, 256, (G, C - 1, 8))
            elif g == 4:
                d = rng.integers(1, 60, 16); X[q, 4, G - 1, C - 1] = x - d; th[q, 4] = int(np.sum(d)) + 1
            elif g == 5:
                d = rng.integers(1, 30, 16); X[q, 5, 0, 0] = x - d; X[q, 5, j, o] = x - rng.integers(30, 60, 16)
                km[q, 5, 0, ::2] = int(np.argmax(c == 0)); th[q, 5] = 4080; th[q, 5, ::2] = int(np.sum(d))
            else:
                v = np.repeat(np.array([0, 255]), 8); X[q, g, j, o] = v
                th[q, g] = 4080 if g == 0 else int(np.min(np.sum(np.abs(last - v), axis=1)))
    X[:, 3] = 255 - rng.integers(0, 64, (N, G, C, 16)); X[:, 3, :, C - 1] = rng.integers(0, 64, (N, G, 16)); th[:, 3] = rng.integers(2048, 4081, (N, P))
    return pack(X, wt, km, th)
def setup_inputs_spread(rng):
    X, wt, km, th = base(rng)
    X = np.minimum((rng.random((N, 8, G, C, 16)) * np.exp2(rng.integers(0, 9, (N, 8, G, C, 1)))).astype(np.int64), 255)
    wt = np.clip(np.exp2(8 * rng.random(wt.shape)).astype(np.int64), 1, 255); km = np.clip(np.exp2(11 * rng.random(km.shape)).astype(np.int64) - 1, 0, 2047); km[..., ::2] = rng.integers(0, 2048, km[..., ::2].shape)
    th = rng.integers(0, 4081, th.shape)
    return pack(X, wt, km, th)
def setup_inputs_ties(rng):
    X, wt, km, th = base(rng)
    pat = rng.integers(1, 254, (8, 4, 16)); a = rng.integers(0, 4, (N, 8, G, C))
    X = pat[np.arange(8)[None, :, None, None], a] + rng.integers(0, 2, (N, 8, G, C, 16)); th = rng.integers(3, 11, th.shape)
    return pack(X, wt, km, th)
def check_inputs(d):
    bad = []; v = np.asarray(d["gen0"]).astype(np.float32)
    if not np.all((v >= 0) & (v <= 255) & (v == np.floor(v))): bad.append("gen0 holds other numbers than 0 .. 255")
    for k, lo, hi in (("wt", 1, 255), ("km", 0, 2047), ("th", 0, 4080)):
        if np.min(d[k]) < lo or np.max(d[k]) > hi: bad.append("range of " + k)
    return bad
def reference(gen0, wt, km, th):
    B = 8 * N; X = gen0.astype(np.float32).astype(np.int32).reshape(B, 16, W); w = wt.astype(np.int64).reshape(B, 16, 1)
    kl = np.stack([gentries(a) for a in km]).astype(np.int64).reshape(B, RO, P); tl = np.stack([gentries(a) for a in th]).astype(np.int64).reshape(B, 1, P)
    ar = np.arange(G); q = np.arange(C); rows = np.arange(B)[:, None]
    for t in range(RO):
        x = X[:, :, C - 1::C]
        u = np.sum(w * x, axis=1) & (W - 1)
        c = probes(u, kl[:, t][:, None, :])
        pr = np.take_along_axis(X, c.reshape(B, 1, G * P), 2).reshape(B, 16, G, P)
        D = np.sum(np.abs(pr - x[..., None]), axis=1).astype(np.int64)
        best = np.min(np.where(D < tl, D * W + c, BIG), axis=2)
        j = (best & (W - 1)) >> LC; o = best & (C - 1); ok = (best < BIG) & (j > ar)
        acc = np.full((B, G), BIG, np.int64)
        np.minimum.at(acc, (rows, np.where(ok, j, 0)), np.where(ok, (best - (best & (W - 1))) + ar * C + o, BIG))
        got = acc < BIG; cut = np.where(got, 1 + ((acc & (C - 1)) >> 1), 0); ln = C - cut
        root = np.where(got, (acc & (W - 1)) >> LC, ar)
        for _ in range(LG): root = np.take_along_axis(root, root, 1)
        od = np.argsort(root * G + ar, axis=1)
        ls = np.take_along_axis(ln, od, 1); pos = np.zeros((B, G), np.int64)
        np.put_along_axis(pos, od, np.add.accumulate(ls, axis=1) - ls, 1); L = np.sum(ln, axis=1)
        place = np.where(q < cut[..., None], W, pos[..., None] + q - cut[..., None])
        src = np.zeros((B, W + 1), np.int64); np.put_along_axis(src, place.reshape(B, W), np.arange(W)[None, :], 1)
        p = ((ar * L[:, None]) >> LG)[..., None] + q * (1 + (u & (H - 1)))[..., None]
        p = np.where(p >= L[:, None, None], p - L[:, None, None], p)
        col = np.take_along_axis(src, p.reshape(B, W), 1)
        kid = np.take_along_axis(X, col[:, None, :], 2).reshape(N, 8, 16, G, C); nxt = np.empty_like(kid)
        for r in range(N):
            for d in range(N): nxt[d, :, :, r * M:(r + 1) * M] = kid[r, :, :, (d - r) % N::N]
        X = nxt.reshape(B, 16, W)
    return {"y": np.ascontiguousarray(X.reshape(N, 128, G, C)[..., :YC]).reshape(N, 128, G * YC).astype(np.float32).astype(BF)}

@@ -1,0 +1,386 @@
+from concourse.bass import DstId, RemoteDMATransfer
+from concourse.mybir import dt, AluOpType as A, AxisListType, ActivationFunctionType as F
+
+NV = 40
+NS = 64 - NV
+VCH = [2, 2, 2, 1, 1]
+SCH = [8, 5, 5, 4, 2]
+LAYS = 176
+BIG = 16777216
+SC = NV * 8
+
+_F32 = [("wtf", 1), ("kmf", 24), ("thf", 8), ("mdg", 64), ("rst", 64), ("rcol", 1), ("qcol", 4), ("qj", 4), ("iq", 4), ("i64", 4), ("ib", 4), ("defn", 4),
+        ("j64", 64), ("ej", 64), ("jj", 64), ("z64", 64), ("m0", 1), ("m1", 1), ("mm0", 2), ("mm1", 2), ("c16", 256), ("kp", 64), ("th4", 512),
+        ("nx", 64), ("uk", 512), ("nk0", 128), ("nk1", 128), ("mk0", 128), ("mk1", 128), ("nks", 8 * NS), ("mks", 8 * NS), ("tm0", NV), ("tm1", NV),
+        ("ta", 4 * NS), ("tb", 2 * NS), ("bk", 64), ("t1", 64), ("bst", 4), ("t0", 4), ("jf", 4), ("okc", 4), ("tt1", 4), ("pk", 4),
+        ("pm0", 128), ("px", 128), ("t2", 128), ("acc", 4), ("got", 4), ("cut", 4), ("pf", 4), ("z", 64), ("zc", 64), ("r1", 64), ("cr", 64), ("er", 64),
+        ("r2", 64), ("r3", 64), ("r4", 64), ("rl", 64), ("sl", 64), ("r8", 64), ("r12", 64), ("r16", 64), ("rl2", 64), ("sl2", 64), ("r32", 64), ("r48", 64),
+        ("kr", 66), ("rl3", 64), ("sl3", 64), ("keyl", 4), ("lenl", 4), ("pm", 64), ("ps", 64), ("mlt", 64), ("x1", 64), ("ww", 64), ("vvv", 64), ("vv", 128),
+        ("dw", 256), ("ls", 256), ("hp", 64), ("qh", 256), ("h63", 64), ("lcol", 1), ("pp", 256), ("pq", 256), ("lp", 64), ("lw", 64), ("lq", 64), ("lm", 64), ("lsc", 64)]
+_I32 = [("wti", 1), ("kmi", 24), ("thi", 8), ("ia", 64), ("ibb", 64), ("icc", 1), ("id4", 4), ("ixo", 2 * NV), ("iu", 128), ("ui", 64), ("um", 64), ("uu", 64), ("vi", 64),
+        ("cp", 512), ("ci", 512), ("bi", 4), ("jb64", 4), ("ai", 4), ("pa", 4), ("oh", 4), ("pi", 64), ("pr", 64), ("p32", 64), ("tl4", 4), ("lsi", 256), ("lsa", 256),
+        ("h31", 64), ("si", 64), ("sp", 64)]
+_BF = [("xa", 4096), ("xb", 4096), ("xl0", 64), ("xl1", 64), ("xl2", 64), ("xp", 4096), ("kb0", 3072), ("kb1", 3072), ("kb2", 1536), ("yb", 2048),
+       ("xk0", 64), ("xk1", 64), ("ones", 128), ("bt", 128), ("blk", 128), ("wb", 128), ("sel", 144), ("nb", 128), ("u0", 128), ("u1", 128), ("b32", 128), ("b3t", 128), ("wm", 128),
+       ("xr", 32 * NV), ("dv0", 32 * NV), ("dv1", 32 * NV), ("av0", 32 * NV), ("av1", 32 * NV), ("as", 128 * NS),
+       ("pl0", 4), ("pl1", 4), ("cl0", 4), ("cl1", 4), ("cc0", 66), ("cc1", 66), ("cc2", 66), ("cc3", 66)]
+_U16 = [("xo", 2 * NV), ("of", 512), ("l1", 4), ("l4", 4), ("l16", 4), ("tl", 8), ("lay", 256), ("kl", 256), ("lx", 4)]
+_PS = ["pu", "pd0", "pd1", "pds", "pv", "plf", "ppos", "pw"]
+_OWN = ("xa", "xb", "xl0", "xl1", "xl2", "kb0", "kb1", "kb2", "yb", "xk0", "xk1", "wti", "kmi", "thi")
+SCRATCH = {}
+PLACE = {}
+for _l, _d, _b, _al in ((_F32, "float32", "ff", 8), (_I32, "int32", "ii", 8), (_BF, "bfloat16", "bb", 16), (_U16, "uint16", "uh", 16)):
+    _at = 0
+    for _n, _w in _l:
+        if _n in _OWN:
+            SCRATCH[_n] = ("sbuf", [128, _w], _d); PLACE[_n] = (_n, 0, _w)
+        else:
+            PLACE[_n] = (_b, _at, _w); _at += (_w + _al - 1) // _al * _al
+    SCRATCH[_b] = ("sbuf", [128, _at], _d)
+for _n in _PS:
+    SCRATCH[_n] = ("psum", [128, 512], "float32"); PLACE[_n] = (_n, 0, 512)
+SEMAPHORES = ["sv", "ss", "st", "sg", "lx0", "lx1", "lw", "lk", "lt", "xs1", "xs2", "stor"] + ["ar%d_%d" % (t, d) for t in range(3) for d in (1, 2, 3)] + ["tx%d" % t for t in range(3)] + ["ux%d" % t for t in range(2)]
+
+
+def rank_program(g, core, T, topo):
+    rank = T.rank_of(core)
+    if rank is None:
+        return
+    n_ranks = len(T.cores)
+    queue = {"v": g.vector, "s": g.scalar, "t": g.tensor, "g": g, "y": g.sync}
+    semname = {"v": "sv", "s": "ss", "t": "st", "g": "sg"}
+    count = {"v": 0, "s": 0, "t": 0, "g": 0}
+    value = {}
+    known = {q: {} for q in queue}
+    snap = {}
+    log = {}
+
+    def D(n, lo=0, hi=None, st=1):
+        b, at, w = PLACE[n]
+        if hi is None: hi = w
+        hi = min(hi, w)
+        return (T[b][:, at + lo:at + hi] if st == 1 else T[b][:, at + lo:at + hi:st], [(n, lo, hi, st)])
+
+    def IND(win, off):
+        return (win[0].indirect(off[0]), win[1] + off[1])
+
+    def meet(a, b):
+        if a[0] >= b[1] or b[0] >= a[1]: return False
+        return not (a[2] == b[2] and a[2] > 1 and (a[0] - b[0]) % a[2] != 0)
+
+    def sync_for(q, outs, ins):
+        need = {}
+        for w, keys in ((True, outs), (False, ins)):
+            for (n, lo, hi, st) in keys:
+                ps = SCRATCH[PLACE[n][0]][0] == "psum"
+                for (src, w2, lo2, hi2, st2), k in log.get(n, {}).items():
+                    hit = (ps and src != q) or ((w or w2) and meet((lo, hi, st), (lo2, hi2, st2)))
+                    if hit and need.get(src, 0) < k: need[src] = k
+        for src, k in need.items():
+            wait(q, src, k)
+
+    def wait(q, src, k):
+        if known[q].get(src, 0) >= k: return
+        queue[q].wait_ge(T.sem[semname[src]], value[(src, k)])
+        for s2, k2 in list(snap[(src, k)].items()) + [(src, k)]:
+            if known[q].get(s2, 0) < k2: known[q][s2] = k2
+
+    def note(src, k, outs, ins):
+        for w, keys in ((True, outs), (False, ins)):
+            for (n, lo, hi, st) in keys:
+                log.setdefault(n, {})[(src, w, lo, hi, st)] = k
+
+    def done(q, ins_):
+        count[q] += 1
+        ins_.then_inc(T.sem[semname[q]], 1)
+        value[(q, count[q])] = count[q]
+        snap[(q, count[q])] = dict(known[q])
+        return count[q]
+
+    def source(name, sem, val, outs):
+        semname[name] = sem
+        value[(name, 1)] = val
+        snap[(name, 1)] = {}
+        note(name, 1, outs, [])
+
+    def col(x):
+        return (x[0], x[1]) if isinstance(x, tuple) else (x, [])
+
+    def run(q, o, i, make):
+        sync_for(q, o[1], i)
+        note(q, done(q, make()), o[1], i)
+
+    def vt(o, a, b, op): run("v", o, a[1] + b[1], lambda: g.vector.tensor_tensor(o[0], a[0], b[0], op))
+
+    def vs(o, a, s1, op0, s2=None, op1=None):
+        c1, k1 = col(s1); c2, k2 = col(s2)
+        if op1 is None: run("v", o, a[1] + k1, lambda: g.vector.tensor_scalar(o[0], a[0], c1, None, op0))
+        else: run("v", o, a[1] + k1 + k2, lambda: g.vector.tensor_scalar(o[0], a[0], c1, c2, op0, op1))
+
+    def vc(o, a): run("v", o, a[1], lambda: g.vector.tensor_copy(o[0], a[0]))
+
+    def vm(o, c): run("v", o, [], lambda: g.vector.memset(o[0], c))
+
+    def vr(o, a, op): run("v", o, a[1], lambda: g.vector.tensor_reduce(o[0], a[0], AxisListType.X, op))
+
+    def vscan(o, a, b, init, op0, op1): run("v", o, a[1] + b[1], lambda: g.vector.tensor_tensor_scan(o[0], a[0], b[0], init, op0, op1))
+
+    def vx(o, a): run("v", o, a[1], lambda: g.vector.transpose(o[0], a[0]))
+
+    def sa(o, a, f, bias=0.0, scale=1.0):
+        c1, k1 = col(bias); c2, k2 = col(scale)
+        run("s", o, a[1] + k1 + k2, lambda: g.scalar.activation(o[0], a[0], f, bias=c1, scale=c2))
+
+    def pe(o, pairs):
+        i = [k for a, b in pairs for k in a[1] + b[1]]
+        sync_for("t", o[1], i)
+        r = None
+        for n, (a, b) in enumerate(pairs):
+            r = g.tensor.matmul(o[0], a[0], b[0], n == 0, n == len(pairs) - 1)
+        note("t", done("t", r), o[1], i)
+
+    def gi(o, pattern, base, cm):
+        if SCRATCH[PLACE[o[1][0][0]][0]][2] == "int32": run("g", o, [], lambda: g.iota(o[0], pattern, base, cm))
+        else: run("g", o, [], lambda: g.iota(o[0], pattern, base, cm, allow_small_or_imprecise_dtypes=True))
+
+    def gsel(o, a, pattern, op, base, cm): run("g", o, a[1], lambda: g.affine_select(o[0], a[0], pattern, op, 0.0, base, cm))
+
+    h = 2048
+    g.sync.dma_start(T.xa[:, 0:h], T.gen0[:, 0:h]).then_inc(T.sem.lx0, 16); source("Lx0", "lx0", 16, D("xa", 0, h)[1])
+    g.scalar.dma_start(T.wti[:], T.wt[:]).then_inc(T.sem.lw, 16); source("Lw", "lw", 16, D("wti")[1])
+    g.scalar.dma_start(T.kmi[:], T.km[:]).then_inc(T.sem.lk, 16); source("Lk", "lk", 16, D("kmi")[1])
+    g.sync.dma_start(T.xa[:, h:4096], T.gen0[:, h:4096]).then_inc(T.sem.lx1, 16); source("Lx1", "lx1", 16, D("xa", h, 4096)[1])
+    g.scalar.dma_start(T.thi[:], T.th[:]).then_inc(T.sem.lt, 16); source("Lt", "lt", 16, D("thi")[1])
+
+    vm(D("ones"), 1.0); vm(D("sel"), 0.0); vm(D("nb"), -131072.0); vm(D("z64"), 0.0); vm(D("c16"), 16.0); vm(D("kr"), 1000000.0); vm(D("dw"), 0.0)
+    gsel(D("bt"), D("ones"), [[-16, 8], [0, 16]], A.is_ge, 0, 1)
+    gsel(D("blk"), D("bt"), [[16, 8], [0, 16]], A.is_ge, 15, -1)
+    gi(D("ixo"), [[0, 2], [1, NV]], 0, 0)
+    gi(D("ia"), [[1, 64]], 128, -1); gi(D("ibb"), [[1, 64]], 0, 0); gi(D("icc"), [[0, 1]], 0, 1)
+    gi(D("iq"), [[16, 4]], 0, 0); gi(D("id4"), [[0, 4]], 0, 64); gi(D("ib"), [[2048, 2], [0, 2]], 0, 0)
+    gi(D("j64"), [[64, 64]], 0, 0)
+    gi(D("kp", 0, 48), [[1, 3], [4, 16]], 1, 0); gi(D("kp", 48, 64), [[4, 16]], 0, 0)
+    gsel(D("b3t"), D("ones"), [[-32, 4], [0, 32]], A.is_ge, 0, 1)
+    gsel(D("b32"), D("b3t"), [[32, 4], [0, 32]], A.is_ge, 31, -1)
+    gi(D("iu"), [[1, 128]], 128, -1)
+    vs(D("sel", 15, 143, 16), D("blk", 0, 128, 16), 4096.0, A.mult)
+    vc(D("xo"), D("ixo"))
+    vc(D("wtf"), D("wti")); vs(D("wb"), D("blk"), D("wtf"), A.mult)
+    vc(D("kmf"), D("kmi"))
+    vs(D("ui"), D("ia"), 15, A.bitwise_and); vs(D("mdg"), D("ui"), 0.0, A.is_equal)
+    vs(D("um"), D("ibb"), 15, A.bitwise_and); vs(D("rst"), D("um"), 0.0, A.not_equal)
+    vs(D("jj"), D("ibb"), 0.015625, A.mult)
+    vs(D("pi", 0, 1), D("icc"), 15, A.bitwise_and); vc(D("rcol"), D("pi", 0, 1))
+    vs(D("pr", 0, 1), D("icc"), 4, A.logical_shift_right, 1, A.bitwise_and); vc(D("m1"), D("pr", 0, 1)); vs(D("m0"), D("m1"), -1.0, A.mult, 1.0, A.add)
+    vs(D("mm0"), D("z64", 0, 2), D("m0"), A.add); vs(D("mm1"), D("z64", 0, 2), D("m1"), A.add)
+    vs(D("qcol"), D("iq"), D("rcol"), A.add); vs(D("qj"), D("qcol"), 0.015625, A.mult)
+    vs(D("bi"), D("id4"), 2047, A.bitwise_and); vt(D("i64"), D("bi"), D("ib"), A.add); vs(D("defn"), D("i64"), -4096.0, A.add)
+    vs(D("ej"), D("j64"), D("rcol"), A.add)
+    vs(D("ci", 0, 128), D("iu"), 15, A.bitwise_and); vs(D("wm"), D("ci", 0, 128), 0.0, A.is_equal)
+    vt(D("u0"), D("wm"), D("b32"), A.mult); vt(D("u1"), D("wm"), D("b32"), A.mult)
+    for a in range(4):
+        vm(D("u0", 32 * a + 16, 32 * a + 32), 0.0); vm(D("u1", 32 * a, 32 * a + 16), 0.0)
+    vs(D("thf"), D("thi"), 4096.0, A.mult, float(-BIG), A.add)
+    for m in range(8):
+        vs(D("th4", m * NV, m * NV + NV), D("z64", 0, NV), D("thf", m, m + 1), A.add)
+        sa(D("th4", SC + m, 512, 8), D("z64", 0, NS), F.Identity, D("thf", m, m + 1))
+
+    for t in range(3):
+        last = t == 2
+        X = "xb" if t == 1 else "xa"
+        XL = "xl%d" % t
+        if t == 0: vc(D(XL), D(X, 63, 4096, 64))
+        pe(D("pu", 0, 64), [(D("wb"), D(XL))])
+        sa(D("xr"), IND(D(XL), D("xo")), F.Copy)
+        vc(D("ui"), D("pu", 0, 64)); vs(D("um"), D("ui"), 4095, A.bitwise_and)
+        vt(D("uu"), D("um"), D("um"), A.mult); vs(D("vi"), D("uu"), 5, A.logical_shift_right)
+
+        def lists(ms):
+            for m in ms: vs(D("uk", m * NV, m * NV + NV), D("um", 0, NV), D("kmf", t * 8 + m, t * 8 + m + 1), A.mult)
+            for m in ms: vt(D("cp", m * NV, m * NV + NV), D("uk", m * NV, m * NV + NV), D("vi", 0, NV), A.add)
+            lo, hi = ms[0] * NV, ms[-1] * NV + NV
+            vs(D("ci", lo, hi), D("cp", lo, hi), 4095, A.bitwise_and); vc(D("of", lo, hi), D("ci", lo, hi))
+        lists([0, 1])
+        vs(D("nx"), D(XL), -1.0, A.mult)
+        for m in range(8): vs(D("uk", SC + m, 512, 8), D("um", NV, 64), D("kmf", t * 8 + m, t * 8 + m + 1), A.mult)
+        for m in range(8): vt(D("cp", SC + m, 512, 8), D("uk", SC + m, 512, 8), D("vi", NV, 64), A.add)
+        vs(D("ci", SC, 512), D("cp", SC, 512), 4095, A.bitwise_and); vc(D("of", SC, 512), D("ci", SC, 512))
+        nq = 2 if last else 4
+
+        def strides():
+            vs(D("h31"), D("um"), 31, A.bitwise_and)
+            for k in range(4): vs(D("hp", 16 * k, 16 * k + 16), D("h31", (k + 1) % 4, 64, 4), 1.0, A.add)
+            for k in range(nq): vs(D("qh", k, 64 * nq, nq), D("hp"), D("qcol", k, k + 1), A.mult)
+            if not last: vs(D("h63"), D("hp"), 63.0, A.mult)
+        if t > 0:
+            lists(list(range(2, 8)))
+            strides()
+        st = {"s": 0, "grp": 0}
+
+        def scalar_genomes(n):
+            for i in range(st["s"], st["s"] + n):
+                sa(D("as", i * 128, i * 128 + 128), IND(D(X), D("of", SC + 8 * i, SC + 8 * i + 8)), F.Abs, D("nx", NV + i, NV + i + 1))
+            st["s"] += n
+            while st["grp"] * 8 + 8 <= st["s"]:
+                q = st["grp"]
+                pe(D("pds", q * 64, q * 64 + 64), [(D("nb"), D("ones", 0, 64))] + [(D("sel", 15 - r, 143 - r), D("as", q * 1024 + r, q * 1024 + 1024, 16)) for r in range(16)])
+                st["grp"] += 1
+
+        def post(P, lo, n, nk, mk):
+            vt(nk, D(P, 0, n), D("ci", lo, lo + n), A.add)
+            vt(D("pv", 0, n), D(P, 0, n), D("th4", lo, lo + n), A.is_lt)
+            vt(mk, D("pv", 0, n), nk, A.mult)
+
+        def postv(c):
+            m0 = sum(VCH[:c]); n = VCH[c] * NV; e = c % 2
+            post("pd%d" % e, m0 * NV, n, D("nk%d" % e, 0, n), D("mk%d" % e, 0, n))
+            mk = "mk%d" % e
+            if VCH[c] == 2:
+                o = D("bk", 0, NV) if c == 0 else D("tm%d" % e)
+                vt(o, D(mk, 0, NV), D(mk, NV, 2 * NV), A.min)
+                if c: vt(D("bk", 0, NV), D("bk", 0, NV), D("tm%d" % e), A.min)
+            else:
+                vt(D("bk", 0, NV), D("bk", 0, NV), D(mk, 0, NV), A.min)
+        for c in range(len(VCH)):
+            m0 = sum(VCH[:c]); n = VCH[c] * NV; e = c % 2
+            vt(D("dv%d" % e, 0, 16 * n), IND(D(X), D("of", m0 * NV, m0 * NV + n)), D("xr", 0, 16 * n), A.subtract)
+            if t == 0 and c == 0: lists(list(range(2, 8)))
+            if t == 0 and c == 3: strides()
+            scalar_genomes(SCH[c])
+            sa(D("av%d" % e, 0, 16 * n), D("dv%d" % e, 0, 16 * n), F.Abs)
+            pe(D("pd%d" % e, 0, n), [(D("nb"), D("ones", 0, n))] + [(D("sel", 15 - r, 143 - r), D("av%d" % e, r, 16 * n, 16)) for r in range(16)])
+            if c: postv(c - 1)
+        post("pds", SC, 8 * NS, D("nks"), D("mks"))
+        vt(D("ta"), D("mks", 0, 8 * NS, 2), D("mks", 1, 8 * NS, 2), A.min)
+        vt(D("tb"), D("ta", 0, 4 * NS, 2), D("ta", 1, 4 * NS, 2), A.min)
+        vt(D("bk", NV, 64), D("tb", 0, 2 * NS, 2), D("tb", 1, 2 * NS, 2), A.min)
+        postv(len(VCH) - 1)
+        vx(D("t1"), D("bk"))
+        for c in range(4): vr(D("bst", c, c + 1), D("t1", 16 * c, 16 * c + 16), A.min)
+        vc(D("bi"), D("bst")); vt(D("t0"), D("bst"), D("i64"), A.add)
+        vs(D("jb64"), D("bi"), 4032, A.bitwise_and)
+        vt(D("tt1"), D("t0"), D("jb64"), A.subtract); vt(D("okc"), D("jb64"), D("i64"), A.is_gt); vc(D("jf"), D("jb64"))
+        vt(D("pk"), D("tt1"), D("okc"), A.mult)
+        for b in range(2):
+            for s in range(2):
+                c = 2 * b + s
+                vs(D("pm0", 64 * s, 64 * s + 64) if b == 0 else D("pv", 64 * s, 64 * s + 64), D("j64"), D("jf", c, c + 1), A.is_equal, D("pk", c, c + 1), A.mult)
+        vt(D("px"), D("pm0"), D("pv", 0, 128), A.min)
+        vx(D("t2"), D("px"))
+        for b in range(2):
+            for s in range(2):
+                vr(D("acc", 2 * b + s, 2 * b + s + 1), D("t2", 64 * s + 32 * b, 64 * s + 32 * b + 32), A.min)
+        vt(D("ai"), D("acc"), D("defn"), A.min); vs(D("got"), D("acc"), 0.0, A.is_lt)
+        vs(D("pa"), D("ai"), 4032, A.bitwise_and, 6, A.logical_shift_right)
+        vs(D("oh"), D("ai"), 62, A.bitwise_and, 1, A.logical_shift_right)
+        vc(D("pf"), D("pa"))
+        for s in range(2):
+            for x in range(2): vt(D("pl%d" % s, x, 4, 2), D("pa", s, 4, 2), D("mm%d" % x), A.mult)
+        for c in range(4): sa(D("z", 16 * c, 16 * c + 16), D("z64", 0, 16), F.Identity, D("pf", c, c + 1))
+        pe(D("plf", 0, 4), [(D("u0"), D("pl0")), (D("u1"), D("pl1"))])
+        vt(D("cut"), D("oh"), D("got"), A.add)
+        vx(D("r1"), D("z")); vc(D("l1"), D("plf", 0, 4))
+        L1 = D("l1"); L4 = D("l4"); L16 = D("l16")
+        for s in range(2):
+            for x in range(2): sa(D("cl%d" % s, x, 4, 2), D("cut", s, 4, 2), F.Identity, 0.0, D("m%d" % x))
+        for c in range(4): sa(D("zc", 16 * c, 16 * c + 16), D("z64", 0, 16), F.Identity, D("cut", c, c + 1))
+        vc(D("r2"), IND(D("r1"), L1))
+        vc(D("r3"), IND(D("r2"), L1))
+        vt(D("rl"), IND(D("r3"), L1), D("mdg"), A.mult); vc(D("r4"), IND(D("r3"), L1))
+        vscan(D("sl"), D("rst"), D("rl"), 0.0, A.mult, A.add)
+        pe(D("plf", 4, 8), [(D("u0"), D("cl0")), (D("u1"), D("cl1"))])
+        vx(D("cr"), D("zc"))
+        vc(L4, D("sl", 15, 64, 16))
+        vs(D("lenl"), D("plf", 4, 8), -1.0, A.mult, 64.0, A.add)
+        vc(D("r8"), IND(D("r4"), L4))
+        vt(D("er"), D("cr"), D("ej"), A.add)
+        vc(D("r12"), IND(D("r8"), L4))
+        vt(D("rl2"), IND(D("r12"), L4), D("mdg"), A.mult); vc(D("r16"), IND(D("r12"), L4))
+        vscan(D("sl2"), D("rst"), D("rl2"), 0.0, A.mult, A.add)
+        vc(L16, D("sl2", 15, 64, 16))
+        vc(D("r32"), IND(D("r16"), L16))
+        vc(D("r48"), IND(D("r32"), L16))
+        vt(D("rl3"), IND(D("r48"), L16), D("mdg"), A.mult)
+        vt(D("kr", 0, 64), IND(D("r48"), L16), D("jj"), A.add)
+        vscan(D("sl3"), D("rst"), D("rl3"), 0.0, A.mult, A.add)
+        vt(D("keyl"), D("sl3", 15, 64, 16), D("qj"), A.add)
+        for q in range(4): vs(D("cc%d" % q, 0, 65), D("kr", 0, 65), D("keyl", q, q + 1), A.is_gt, D("lenl", q, q + 1), A.mult)
+        pe(D("ppos", 0, 65), [(D("blk"), D("cc%d" % q, 0, 65)) for q in range(4)])
+        vt(D("pm"), D("ppos", 0, 64), D("mdg"), A.mult)
+        vc(D("pi"), D("ppos", 0, 64))
+        vscan(D("ps"), D("rst"), D("pm"), 0.0, A.mult, A.add)
+        vs(D("pr"), D("pi"), 15, A.bitwise_and); vs(D("p32"), D("pi"), 4064, A.bitwise_and)
+        vs(D("tl4"), D("ps", 15, 64, 16), 0.0625, A.mult, -0.46875, A.add)
+        vt(D("x1"), D("er"), D("pr"), A.subtract); vs(D("ww"), D("p32"), 128.0, A.mult)
+        vc(D("tl", 0, 4), D("tl4")); vs(D("tl", 4, 8), D("tl4"), 1.0, A.add)
+        vs(D("mlt"), D("pr"), D("rcol"), A.is_le); vt(D("vvv"), D("x1"), D("ww"), A.add)
+        vc(D("lcol"), D("ppos", 64, 65))
+        vt(D("vv", 0, 64), D("vvv"), D("mlt"), A.mult); vs(D("vv", 64, 128), D("vvv"), 16.0, A.add)
+        vs(D("si"), D("kp"), D("lcol"), A.mult)
+        vc(IND(D("dw"), D("tl")), D("vv"))
+        vs(D("sp"), D("si"), 6, A.logical_shift_right)
+        vscan(D("ls"), D("c16"), D("dw"), -1000.0, A.add, A.max)
+        for a in range(2):
+            lo, hi = 128 * a, 128 * a + 128
+            vc(D("lsi", lo, hi), D("ls", lo, hi)); vs(D("lsa", lo, hi), D("lsi", lo, hi), 4095, A.bitwise_and); vc(D("lay", lo, hi), D("lsa", lo, hi))
+        sa(D("xp", 0, 2048), IND(D(X), D("lay", 0, 128)), F.Copy)
+        sa(D("xp", 2048, 16 * LAYS), IND(D(X), D("lay", 128, LAYS)), F.Copy)
+        if not last: vt(D("lp"), D("h63"), D("sp"), A.add)
+        for k in range(nq): vt(D("pp", k, 64 * nq, nq), D("qh", k, 64 * nq, nq), D("sp"), A.add)
+        if not last:
+            vs(D("lw"), D("lp"), D("lcol"), A.is_ge, D("lcol"), A.mult)
+        vs(D("pv", 0, 64 * nq), D("pp", 0, 64 * nq), D("lcol"), A.is_ge, D("lcol"), A.mult)
+        if not last: vt(D("lq"), D("lp"), D("lw"), A.subtract)
+        vt(D("pq", 0, 64 * nq), D("pp", 0, 64 * nq), D("pv", 0, 64 * nq), A.subtract)
+        if not last: vt(D("lm"), D("lq"), D("mdg"), A.mult)
+        vc(D("kl", 0, 64 * nq), D("pq", 0, 64 * nq))
+        if not last: vscan(D("lsc"), D("rst"), D("lm"), 0.0, A.mult, A.add)
+        vc(D("xp", 16 * LAYS, 4096), IND(D(X), D("lay", LAYS, 256)))
+        if not last: vc(D("lx"), D("lsc", 15, 64, 16))
+        w = 256 * nq
+        XN = "yb" if last else ("xa" if t == 1 else "xb")
+        KB = "kb%d" % t
+        if not last:
+            XK = "xk%d" % t; XLN = "xl%d" % (t + 1)
+            vc(D(XK), IND(D("xp"), D("lx")))
+            sync_for("g", [], D(XK, 0, 48)[1])
+            trs = []
+            for k in range(3):
+                d = T.cores[(rank + k + 1) % n_ranks]
+                rid, pid = topo.addr(d, core)
+                en = topo.engines(core, d)
+                mask = (1 << en[2 * k]) + (1 << en[2 * k + 1])
+                trs.append(RemoteDMATransfer(dst_ids=[DstId(rid=rid, pnc=pid)], dma_engine_mask=mask, remote_sem=T.sem["xs%d" % (t + 1)],
+                                             src=T[XK][:, 16 * k:16 * k + 16], dst=T[XLN][:, 16 * rank:16 * rank + 16]))
+            g.remote_dma_fused(trs, local_sem=T.sem["ux%d" % t])
+            for k in range(1, 4):
+                p = (rank - k) % n_ranks
+                source("XS%d" % (t + 1), "xs%d" % (t + 1), 6, D(XLN, 16 * p, 16 * p + 16)[1])
+        for k in range(4):
+            n = w // 32
+            if k < 3: oa = D(KB, k * w, k * w + w // 2); ob = D(KB, k * w + w // 2, k * w + w)
+            else: oa = D(XN, rank * w, rank * w + w // 2); ob = D(XN, rank * w + w // 2, rank * w + w)
+            vc(oa, IND(D("xp"), D("kl", 2 * k * n, 2 * k * n + n)))
+            sa(ob, IND(D("xp"), D("kl", 2 * k * n + n, 2 * k * n + 2 * n)), F.Copy)
+            if k < 3:
+                d = T.cores[(rank + k + 1) % n_ranks]
+                rid, pid = topo.addr(d, core)
+                sync_for("g", [], D(KB, k * w, k * w + w)[1])
+                g.remote_dma(T[XN][:, rank * w:rank * w + w], T[KB][:, k * w:k * w + w], T.sem["ar%d_%d" % (t, k + 1)], T.sem["tx%d" % t], pid, rid, topo.mask(core, d))
+        if not last:
+            vc(D(XLN, 16 * rank, 16 * rank + 16), D(XK, 48, 64))
+            vm(D("dw"), 0.0)
+        for k in range(1, 4):
+            p = (rank - k) % n_ranks
+            source("AR%d_%d" % (t, k), "ar%d_%d" % (t, k), len(topo.engines(T.cores[p], core)), D(XN, p * w, p * w + w)[1])
+
+    for k in range(4):
+        p = (rank - k) % n_ranks
+        sync_for("y", [], D("yb", p * 512, p * 512 + 512)[1])
+        g.sync.dma_start(T.y[:, p * 512:p * 512 + 512], T.yb[:, p * 512:p * 512 + 512]).then_inc(T.sem.stor, 16)
+    g.sync.wait_ge(T.sem.stor, 64)
+    for t in range(3):
+        g.wait_ge(T.sem["tx%d" % t], sum(len(topo.engines(core, T.cores[(rank + k) % n_ranks])) for k in (1, 2, 3)))
+        if t < 2: g.wait_ge(T.sem["ux%d" % t], 6)
+    for q in ("v", "s", "t", "g"):
+        wait("g", q, count[q])

@@ -1,29 +1,34 @@
 from concourse.bass import DstId, RemoteDMATransfer
 from concourse.mybir import dt, AluOpType as A, AxisListType, ActivationFunctionType as F
 
-NV = 40
+NV = 38
 NS = 64 - NV
 VCH = [2, 2, 2, 1, 1]
-SCH = [8, 5, 5, 4, 2]
-LAYS = 176
+SCH = [7, 3, 2, NS - 12, 0]
+SGR = [8, 8, NS - 16]
+RELU = (3, 4)
+RELAY = ((0, 1), (0, 1), ())
+LAYS = (162, 162, 148)
 BIG = 16777216
 SC = NV * 8
 
-_F32 = [("wtf", 1), ("kmf", 24), ("thf", 8), ("mdg", 64), ("rst", 64), ("rcol", 1), ("qcol", 4), ("qj", 4), ("iq", 4), ("i64", 4), ("ib", 4), ("defn", 4),
-        ("j64", 64), ("ej", 64), ("jj", 64), ("z64", 64), ("m0", 1), ("m1", 1), ("mm0", 2), ("mm1", 2), ("c16", 256), ("kp", 64), ("th4", 512),
-        ("nx", 64), ("uk", 512), ("nk0", 128), ("nk1", 128), ("mk0", 128), ("mk1", 128), ("nks", 8 * NS), ("mks", 8 * NS), ("tm0", NV), ("tm1", NV),
-        ("ta", 4 * NS), ("tb", 2 * NS), ("bk", 64), ("t1", 64), ("bst", 4), ("t0", 4), ("jf", 4), ("okc", 4), ("tt1", 4), ("pk", 4),
-        ("pm0", 128), ("px", 128), ("t2", 128), ("acc", 4), ("got", 4), ("cut", 4), ("pf", 4), ("z", 64), ("zc", 64), ("r1", 64), ("cr", 64), ("er", 64),
+_F32 = [("wtf", 1), ("kmf", 24), ("thf", 8), ("mdg", 64), ("rst", 64), ("rcol", 1), ("qcol", 4), ("qj", 4), ("iq", 4), ("i64", 4), ("ib", 4), ("idf", 4), ("df", 4), ("defn", 4),
+        ("s16", 64), ("s32", 128), ("j64", 64), ("ej", 64), ("jj", 64), ("z64", 64), ("m0", 1), ("m1", 1), ("mm0", 4), ("mm1", 4), ("c16", 256), ("kp", 64), ("th4", 512),
+        ("nx", 64), ("uk", 512), ("nk", 512), ("mk", 512), ("tm0", 2 * NV), ("tm1", NV),
+        ("ta", 4 * NS), ("tb", 2 * NS), ("bk", 64), ("t1", 64), ("bsc", 64), ("t0", 4), ("jf", 4), ("okc", 4), ("tt1", 4), ("pk", 4),
+        ("pm0", 128), ("px", 128), ("t2", 128), ("acs", 128), ("got", 4), ("cut", 4), ("pf", 4), ("z", 64), ("zc", 64), ("r1", 64), ("cr", 64), ("er", 64),
         ("r2", 64), ("r3", 64), ("r4", 64), ("rl", 64), ("sl", 64), ("r8", 64), ("r12", 64), ("r16", 64), ("rl2", 64), ("sl2", 64), ("r32", 64), ("r48", 64),
         ("kr", 66), ("rl3", 64), ("sl3", 64), ("keyl", 4), ("lenl", 4), ("pm", 64), ("ps", 64), ("mlt", 64), ("x1", 64), ("ww", 64), ("vvv", 64), ("vv", 128),
-        ("dw", 256), ("ls", 256), ("hp", 64), ("qh", 256), ("h63", 64), ("lcol", 1), ("pp", 256), ("pq", 256), ("lp", 64), ("lw", 64), ("lq", 64), ("lm", 64), ("lsc", 64)]
+        ("dw", 256), ("ls", 256), ("hp", 64), ("h63", 64), ("lcol", 1), ("pp", 256), ("pq", 256), ("lp", 64), ("lw", 64), ("lq", 64), ("lm", 64), ("lsc", 64)]
 _I32 = [("wti", 1), ("kmi", 24), ("thi", 8), ("ia", 64), ("ibb", 64), ("icc", 1), ("id4", 4), ("ixo", 2 * NV), ("iu", 128), ("ui", 64), ("um", 64), ("uu", 64), ("vi", 64),
         ("cp", 512), ("ci", 512), ("bi", 4), ("jb64", 4), ("ai", 4), ("pa", 4), ("oh", 4), ("pi", 64), ("pr", 64), ("p32", 64), ("tl4", 4), ("lsi", 256), ("lsa", 256),
         ("h31", 64), ("si", 64), ("sp", 64)]
 _BF = [("xa", 4096), ("xb", 4096), ("xl0", 64), ("xl1", 64), ("xl2", 64), ("xp", 4096), ("kb0", 3072), ("kb1", 3072), ("kb2", 1536), ("yb", 2048),
-       ("xk0", 64), ("xk1", 64), ("ones", 128), ("bt", 128), ("blk", 128), ("wb", 128), ("sel", 144), ("nb", 128), ("u0", 128), ("u1", 128), ("b32", 128), ("b3t", 128), ("wm", 128),
-       ("xr", 32 * NV), ("dv0", 32 * NV), ("dv1", 32 * NV), ("av0", 32 * NV), ("av1", 32 * NV), ("as", 128 * NS),
-       ("pl0", 4), ("pl1", 4), ("cl0", 4), ("cl1", 4), ("cc0", 66), ("cc1", 66), ("cc2", 66), ("cc3", 66)]
+       ("xk0", 64), ("xk1", 64), ("ones", 128), ("bt", 128), ("blk", 128), ("wb", 128), ("sel", 144), ("sel2", 144), ("seln", 144), ("nb", 128),
+       ("u0", 128), ("u1", 128), ("b32", 128), ("b3t", 128), ("wm", 128), ("wm2", 128),
+       ("xr", 32 * NV), ("dv0", 32 * NV), ("dv1", 32 * NV), ("dv2", 32 * NV), ("av0", 32 * NV), ("av1", 32 * NV), ("av2", 32 * NV),
+       ("rv0", 32 * NV), ("rv1", 32 * NV), ("rv2", 32 * NV), ("as", 128 * NS),
+       ("pl", 8), ("cl", 8), ("cc0", 66), ("cc1", 66), ("cc2", 66), ("cc3", 66)]
 _U16 = [("xo", 2 * NV), ("of", 512), ("l1", 4), ("l4", 4), ("l16", 4), ("tl", 8), ("lay", 256), ("kl", 256), ("lx", 4)]
 _PS = ["pu", "pd0", "pd1", "pds", "pv", "plf", "ppos", "pw"]
 _OWN = ("xa", "xb", "xl0", "xl1", "xl2", "kb0", "kb1", "kb2", "yb", "xk0", "xk1", "wti", "kmi", "thi")
@@ -39,20 +44,44 @@ for _l, _d, _b, _al in ((_F32, "float32", "ff", 8), (_I32, "int32", "ii", 8), (_
     SCRATCH[_b] = ("sbuf", [128, _at], _d)
 for _n in _PS:
     SCRATCH[_n] = ("psum", [128, 512], "float32"); PLACE[_n] = (_n, 0, 512)
-SEMAPHORES = ["sv", "ss", "st", "sg", "lx0", "lx1", "lw", "lk", "lt", "xs1", "xs2", "stor"] + ["ar%d_%d" % (t, d) for t in range(3) for d in (1, 2, 3)] + ["tx%d" % t for t in range(3)] + ["ux%d" % t for t in range(2)]
+SEMAPHORES = ["sv", "ss", "st", "sg", "lx0", "lx1", "lw", "lk", "lt", "xs1", "xs2", "stor"] + ["ra%d" % t for t in range(3)]
+SEMAPHORES += ["ar%d_%d" % (t, d) for t in range(3) for d in (1, 2, 3)] + ["tx%d" % t for t in range(3)] + ["ux%d" % t for t in range(2)]
 
 
 def rank_program(g, core, T, topo):
+    n_ranks = len(T.cores)
+
+    def helpers(rc):
+        return [c for c in topo.cores_of(rc) if topo.die(c) != topo.die(rc) and all(topo.may_write(c, d) for d in T.cores)]
+
+    def hop_engines(rc, hc, d):
+        off = topo.engines(rc, d)
+        return [e for e in topo.engines(rc, hc) if e not in off]
+
+    def width(t):
+        return 512 if t == 2 else 1024
     rank = T.rank_of(core)
     if rank is None:
+        for r, rc in enumerate(T.cores):
+            hs = helpers(rc)
+            if core not in hs: continue
+            k = hs.index(core)
+            for t in range(3):
+                if k not in RELAY[t]: continue
+                d = T.cores[(r + k + 1) % n_ranks]
+                rid, pid = topo.addr(d, core)
+                w = width(t); KB = "kb%d" % t; XN = "xa" if t == 1 else "xb" if t == 0 else "yb"
+                g.wait_ge(T.sem["ra%d" % t], len(hop_engines(rc, core, d)))
+                g.remote_dma(T[XN][:, r * w + w // 2:r * w + w], T[KB][:, k * w + w // 2:k * w + w], T.sem["ar%d_%d" % (t, k + 1)], T.sem["tx%d" % t], pid, rid, topo.mask(core, d))
+                g.wait_ge(T.sem["tx%d" % t], len(topo.engines(core, d)))
         return
-    n_ranks = len(T.cores)
     queue = {"v": g.vector, "s": g.scalar, "t": g.tensor, "g": g, "y": g.sync}
     semname = {"v": "sv", "s": "ss", "t": "st", "g": "sg"}
     count = {"v": 0, "s": 0, "t": 0, "g": 0}
     value = {}
     known = {q: {} for q in queue}
     snap = {}
+    sent = [0, 0, 0]
     log = {}
 
     def D(n, lo=0, hi=None, st=1):
@@ -121,8 +150,6 @@ def rank_program(g, core, T, topo):
 
     def vm(o, c): run("v", o, [], lambda: g.vector.memset(o[0], c))
 
-    def vr(o, a, op): run("v", o, a[1], lambda: g.vector.tensor_reduce(o[0], a[0], AxisListType.X, op))
-
     def vscan(o, a, b, init, op0, op1): run("v", o, a[1] + b[1], lambda: g.vector.tensor_tensor_scan(o[0], a[0], b[0], init, op0, op1))
 
     def vx(o, a): run("v", o, a[1], lambda: g.vector.transpose(o[0], a[0]))
@@ -131,12 +158,15 @@ def rank_program(g, core, T, topo):
         c1, k1 = col(bias); c2, k2 = col(scale)
         run("s", o, a[1] + k1 + k2, lambda: g.scalar.activation(o[0], a[0], f, bias=c1, scale=c2))
 
-    def pe(o, pairs):
-        i = [k for a, b in pairs for k in a[1] + b[1]]
-        sync_for("t", o[1], i)
+    def pe(o, *parts):
+        i = []
         r = None
-        for n, (a, b) in enumerate(pairs):
-            r = g.tensor.matmul(o[0], a[0], b[0], n == 0, n == len(pairs) - 1)
+        for p, pairs in enumerate(parts):
+            j = [k for a, b in pairs for k in a[1] + b[1]]
+            sync_for("t", o[1] if p == 0 else [], j)
+            i = i + j
+            for n, (a, b) in enumerate(pairs):
+                r = g.tensor.matmul(o[0], a[0], b[0], p == 0 and n == 0, p == len(parts) - 1 and n == len(pairs) - 1)
         note("t", done("t", r), o[1], i)
 
     def gi(o, pattern, base, cm):
@@ -152,38 +182,45 @@ def rank_program(g, core, T, topo):
     g.sync.dma_start(T.xa[:, h:4096], T.gen0[:, h:4096]).then_inc(T.sem.lx1, 16); source("Lx1", "lx1", 16, D("xa", h, 4096)[1])
     g.scalar.dma_start(T.thi[:], T.th[:]).then_inc(T.sem.lt, 16); source("Lt", "lt", 16, D("thi")[1])
 
-    vm(D("ones"), 1.0); vm(D("sel"), 0.0); vm(D("nb"), -131072.0); vm(D("z64"), 0.0); vm(D("c16"), 16.0); vm(D("kr"), 1000000.0); vm(D("dw"), 0.0)
+    vm(D("ones"), 1.0); vm(D("sel"), 0.0)
+    gi(D("z64"), [[0, 64]], 0, 0)
     gsel(D("bt"), D("ones"), [[-16, 8], [0, 16]], A.is_ge, 0, 1)
     gsel(D("blk"), D("bt"), [[16, 8], [0, 16]], A.is_ge, 15, -1)
+    gi(D("icc"), [[0, 1]], 0, 1); gi(D("ibb"), [[1, 64]], 0, 0); gi(D("ia"), [[1, 64]], 128, -1)
     gi(D("ixo"), [[0, 2], [1, NV]], 0, 0)
-    gi(D("ia"), [[1, 64]], 128, -1); gi(D("ibb"), [[1, 64]], 0, 0); gi(D("icc"), [[0, 1]], 0, 1)
-    gi(D("iq"), [[16, 4]], 0, 0); gi(D("id4"), [[0, 4]], 0, 64); gi(D("ib"), [[2048, 2], [0, 2]], 0, 0)
-    gi(D("j64"), [[64, 64]], 0, 0)
-    gi(D("kp", 0, 48), [[1, 3], [4, 16]], 1, 0); gi(D("kp", 48, 64), [[4, 16]], 0, 0)
+    gi(D("j64"), [[64, 64]], 0, 0); gi(D("iq"), [[16, 4]], 0, 0)
+    gi(D("id4"), [[0, 4]], 0, 64); gi(D("ib"), [[2048, 2], [0, 2]], 0, 0); gi(D("idf"), [[0, 2], [2048, 2]], 0, 0)
+    gi(D("iu"), [[1, 128]], 128, -1)
     gsel(D("b3t"), D("ones"), [[-32, 4], [0, 32]], A.is_ge, 0, 1)
     gsel(D("b32"), D("b3t"), [[32, 4], [0, 32]], A.is_ge, 31, -1)
-    gi(D("iu"), [[1, 128]], 128, -1)
+    gi(D("nb"), [[0, 128]], -131072, 0)
+    vc(D("wtf"), D("wti")); vc(D("kmf"), D("kmi")); vs(D("thf"), D("thi"), 4096.0, A.mult, float(-BIG), A.add)
     vs(D("sel", 15, 143, 16), D("blk", 0, 128, 16), 4096.0, A.mult)
+    vs(D("wb"), D("blk"), D("wtf"), A.mult)
+    vs(D("pi", 0, 1), D("icc"), 15, A.bitwise_and); vs(D("pr", 0, 1), D("icc"), 4, A.logical_shift_right, 1, A.bitwise_and)
+    vc(D("rcol"), D("pi", 0, 1)); vc(D("m1"), D("pr", 0, 1))
+    vs(D("um"), D("ibb"), 15, A.bitwise_and); vs(D("ui"), D("ia"), 15, A.bitwise_and)
+    vs(D("rst"), D("um"), 0.0, A.not_equal); vs(D("mdg"), D("ui"), 0.0, A.is_equal)
     vc(D("xo"), D("ixo"))
-    vc(D("wtf"), D("wti")); vs(D("wb"), D("blk"), D("wtf"), A.mult)
-    vc(D("kmf"), D("kmi"))
-    vs(D("ui"), D("ia"), 15, A.bitwise_and); vs(D("mdg"), D("ui"), 0.0, A.is_equal)
-    vs(D("um"), D("ibb"), 15, A.bitwise_and); vs(D("rst"), D("um"), 0.0, A.not_equal)
-    vs(D("jj"), D("ibb"), 0.015625, A.mult)
-    vs(D("pi", 0, 1), D("icc"), 15, A.bitwise_and); vc(D("rcol"), D("pi", 0, 1))
-    vs(D("pr", 0, 1), D("icc"), 4, A.logical_shift_right, 1, A.bitwise_and); vc(D("m1"), D("pr", 0, 1)); vs(D("m0"), D("m1"), -1.0, A.mult, 1.0, A.add)
-    vs(D("mm0"), D("z64", 0, 2), D("m0"), A.add); vs(D("mm1"), D("z64", 0, 2), D("m1"), A.add)
-    vs(D("qcol"), D("iq"), D("rcol"), A.add); vs(D("qj"), D("qcol"), 0.015625, A.mult)
-    vs(D("bi"), D("id4"), 2047, A.bitwise_and); vt(D("i64"), D("bi"), D("ib"), A.add); vs(D("defn"), D("i64"), -4096.0, A.add)
-    vs(D("ej"), D("j64"), D("rcol"), A.add)
-    vs(D("ci", 0, 128), D("iu"), 15, A.bitwise_and); vs(D("wm"), D("ci", 0, 128), 0.0, A.is_equal)
-    vt(D("u0"), D("wm"), D("b32"), A.mult); vt(D("u1"), D("wm"), D("b32"), A.mult)
-    for a in range(4):
-        vm(D("u0", 32 * a + 16, 32 * a + 32), 0.0); vm(D("u1", 32 * a, 32 * a + 16), 0.0)
-    vs(D("thf"), D("thi"), 4096.0, A.mult, float(-BIG), A.add)
+    vs(D("bi"), D("id4"), 2047, A.bitwise_and); vs(D("ci", 0, 128), D("iu"), 15, A.bitwise_and)
+    vt(D("i64"), D("bi"), D("ib"), A.add); vt(D("df"), D("bi"), D("idf"), A.add); vs(D("wm"), D("ci", 0, 128), 0.0, A.is_equal)
+    vs(D("defn"), D("df"), -4096.0, A.add)
+    vm(D("s32"), float(-2 * BIG)); vm(D("s32", 0, 128, 32), 1.0)
+    vt(D("wm2"), D("wm"), D("b32"), A.mult)
+    vm(D("dw"), 0.0)
+    sa(D("sel2"), D("sel"), F.Copy, 0.0, 2.0); sa(D("seln"), D("sel"), F.Copy, 0.0, -1.0)
+    sa(D("m0"), D("m1"), F.Copy, 1.0, -1.0)
+    sa(D("mm1"), D("z64", 0, 4), F.Identity, D("m1")); sa(D("mm0"), D("z64", 0, 4), F.Identity, D("m0"))
+    sa(D("s16"), D("rst"), F.Copy, 1.0, float(-2 * BIG))
+    sa(D("jj"), D("j64"), F.Copy, 0.0, 1.0 / 4096); sa(D("ej"), D("j64"), F.Identity, D("rcol"))
+    sa(D("qcol"), D("iq"), F.Identity, D("rcol")); sa(D("qj"), D("qcol"), F.Copy, 0.0, 0.015625)
     for m in range(8):
-        vs(D("th4", m * NV, m * NV + NV), D("z64", 0, NV), D("thf", m, m + 1), A.add)
+        sa(D("th4", m * NV, m * NV + NV), D("z64", 0, NV), F.Identity, D("thf", m, m + 1))
         sa(D("th4", SC + m, 512, 8), D("z64", 0, NS), F.Identity, D("thf", m, m + 1))
+    gsel(D("u0"), D("wm2"), [[0, 4], [1, 2], [0, 16]], A.is_equal, 0, 0)
+    gsel(D("u1"), D("wm2"), [[0, 4], [1, 2], [0, 16]], A.is_gt, 0, 0)
+    gi(D("kr"), [[0, 66]], 1000000, 0); gi(D("c16"), [[0, 256]], 16, 0)
+    gi(D("kp", 0, 48), [[1, 3], [4, 16]], 1, 0); gi(D("kp", 48, 64), [[4, 16]], 0, 0)
 
     for t in range(3):
         last = t == 2
@@ -210,54 +247,85 @@ def rank_program(g, core, T, topo):
         def strides():
             vs(D("h31"), D("um"), 31, A.bitwise_and)
             for k in range(4): vs(D("hp", 16 * k, 16 * k + 16), D("h31", (k + 1) % 4, 64, 4), 1.0, A.add)
-            for k in range(nq): vs(D("qh", k, 64 * nq, nq), D("hp"), D("qcol", k, k + 1), A.mult)
+            for k in range(nq): vs(D("pw", k, 64 * nq, nq), D("hp"), D("qcol", k, k + 1), A.mult)
             if not last: vs(D("h63"), D("hp"), 63.0, A.mult)
         if t > 0:
             lists(list(range(2, 8)))
             strides()
-        st = {"s": 0, "grp": 0}
+        bank = ["pd0", "pd0", "pd1", "pd1", "pu"]
+        at = [0, 2 * NV, 0, 2 * NV, 0]
+        sbank = ["pds", "pds", "plf"]
+        scol = [0, 8 * SGR[0], 0]
+        m0 = [sum(VCH[:c]) for c in range(5)]
+        s0 = [sum(SGR[:c]) for c in range(4)]
 
-        def scalar_genomes(n):
-            for i in range(st["s"], st["s"] + n):
+        def vgather(c):
+            n = 16 * VCH[c] * NV
+            dv = D("dv%d" % (c % 3), 0, n)
+            vt(dv, IND(D(X), D("of", m0[c] * NV, (m0[c] + VCH[c]) * NV)), D("xr", 0, n), A.subtract)
+            if c in RELU: vs(D("rv%d" % (c % 3), 0, n), dv, 0.0, A.max)
+
+        def sgather(c):
+            for i in range(sum(SCH[:c]), sum(SCH[:c + 1])):
                 sa(D("as", i * 128, i * 128 + 128), IND(D(X), D("of", SC + 8 * i, SC + 8 * i + 8)), F.Abs, D("nx", NV + i, NV + i + 1))
-            st["s"] += n
-            while st["grp"] * 8 + 8 <= st["s"]:
-                q = st["grp"]
-                pe(D("pds", q * 64, q * 64 + 64), [(D("nb"), D("ones", 0, 64))] + [(D("sel", 15 - r, 143 - r), D("as", q * 1024 + r, q * 1024 + 1024, 16)) for r in range(16)])
-                st["grp"] += 1
+            if c not in RELU: sa(D("av%d" % (c % 3), 0, 16 * VCH[c] * NV), D("dv%d" % (c % 3), 0, 16 * VCH[c] * NV), F.Abs)
 
-        def post(P, lo, n, nk, mk):
-            vt(nk, D(P, 0, n), D("ci", lo, lo + n), A.add)
-            vt(D("pv", 0, n), D(P, 0, n), D("th4", lo, lo + n), A.is_lt)
-            vt(mk, D("pv", 0, n), nk, A.mult)
+        def sums(s, b, lo, hi):
+            return [(D(s, 15 - r, 143 - r), D(b, lo + r, hi, 16)) for r in range(16)]
 
-        def postv(c):
-            m0 = sum(VCH[:c]); n = VCH[c] * NV; e = c % 2
-            post("pd%d" % e, m0 * NV, n, D("nk%d" % e, 0, n), D("mk%d" % e, 0, n))
-            mk = "mk%d" % e
-            if VCH[c] == 2:
-                o = D("bk", 0, NV) if c == 0 else D("tm%d" % e)
-                vt(o, D(mk, 0, NV), D(mk, NV, 2 * NV), A.min)
-                if c: vt(D("bk", 0, NV), D("bk", 0, NV), D("tm%d" % e), A.min)
-            else:
-                vt(D("bk", 0, NV), D("bk", 0, NV), D(mk, 0, NV), A.min)
-        for c in range(len(VCH)):
-            m0 = sum(VCH[:c]); n = VCH[c] * NV; e = c % 2
-            vt(D("dv%d" % e, 0, 16 * n), IND(D(X), D("of", m0 * NV, m0 * NV + n)), D("xr", 0, 16 * n), A.subtract)
-            if t == 0 and c == 0: lists(list(range(2, 8)))
-            if t == 0 and c == 3: strides()
-            scalar_genomes(SCH[c])
-            sa(D("av%d" % e, 0, 16 * n), D("dv%d" % e, 0, 16 * n), F.Abs)
-            pe(D("pd%d" % e, 0, n), [(D("nb"), D("ones", 0, n))] + [(D("sel", 15 - r, 143 - r), D("av%d" % e, r, 16 * n, 16)) for r in range(16)])
-            if c: postv(c - 1)
-        post("pds", SC, 8 * NS, D("nks"), D("mks"))
-        vt(D("ta"), D("mks", 0, 8 * NS, 2), D("mks", 1, 8 * NS, 2), A.min)
-        vt(D("tb"), D("ta", 0, 4 * NS, 2), D("ta", 1, 4 * NS, 2), A.min)
-        vt(D("bk", NV, 64), D("tb", 0, 2 * NS, 2), D("tb", 1, 2 * NS, 2), A.min)
-        postv(len(VCH) - 1)
+        def vsums(c):
+            n = VCH[c] * NV
+            o = D(bank[c], at[c], at[c] + n)
+            e = c % 3
+            bias = [(D("nb"), D("ones", 0, n))]
+            if c in RELU: pe(o, bias + sums("seln", "dv%d" % e, 0, 16 * n), sums("sel2", "rv%d" % e, 0, 16 * n))
+            else: pe(o, bias + sums("sel", "av%d" % e, 0, 16 * n))
+
+        def ssums(q):
+            n = 8 * SGR[q]
+            pe(D(sbank[q], scol[q], scol[q] + n), [(D("nb"), D("ones", 0, n))] + sums("sel", "as", s0[q] * 128, s0[q + 1] * 128))
+
+        def posts(parts):
+            for P, b, lo, n in parts: vt(D("nk", lo, lo + n), D(P, b, b + n), D("ci", lo, lo + n), A.add)
+            for P, b, lo, n in parts: vt(D("pv", lo, lo + n), D(P, b, b + n), D("th4", lo, lo + n), A.is_lt)
+            for P, b, lo, n in parts: vt(D("mk", lo, lo + n), D("pv", lo, lo + n), D("nk", lo, lo + n), A.mult)
+
+        def smin(q):
+            lo, hi = SC + 8 * s0[q], SC + 8 * s0[q + 1]
+            a, b = s0[q], s0[q + 1]
+            yield vt(D("ta", 4 * a, 4 * b), D("mk", lo, hi, 2), D("mk", lo + 1, hi, 2), A.min)
+            yield vt(D("tb", 2 * a, 2 * b), D("ta", 4 * a, 4 * b, 2), D("ta", 4 * a + 1, 4 * b, 2), A.min)
+            yield vt(D("bk", NV + a, NV + b), D("tb", 2 * a, 2 * b, 2), D("tb", 2 * a + 1, 2 * b, 2), A.min)
+
+        def weave(*gs):
+            for _ in range(4):
+                for x in gs: next(x, None)
+        bv = D("bk", 0, NV)
+
+        def M(m, k=1): return D("mk", m * NV, (m + k) * NV)
+
+        def amin():
+            yield vt(D("tm0"), M(0, 2), M(2, 2), A.min)
+            yield vt(bv, D("tm0", 0, NV), D("tm0", NV, 2 * NV), A.min)
+
+        def bmin():
+            yield vt(D("tm0", 0, NV), M(4), M(5), A.min)
+            yield vt(D("tm1"), D("tm0", 0, NV), M(6), A.min)
+            yield vt(bv, bv, D("tm1"), A.min)
+        vgather(0); sgather(0)
+        if t == 0: lists(list(range(2, 8)))
+        vgather(1); vsums(0); sgather(1); ssums(0)
+        vgather(2); vsums(1); sgather(2); vsums(2); sgather(3)
+        posts([("pd0", 0, 0, 4 * NV)]); weave(amin())
+        vgather(3); vsums(3); ssums(1)
+        if t == 0: strides()
+        vgather(4); vsums(4); ssums(2)
+        posts([("pd1", 0, 4 * NV, 3 * NV), ("pds", 0, SC, 8 * s0[2])]); weave(bmin(), smin(0), smin(1))
+        posts([("pu", 0, 7 * NV, NV), ("plf", 0, SC + 8 * s0[2], 8 * SGR[2])])
+        weave(smin(2), iter([vt(bv, bv, M(7), A.min)]))
         vx(D("t1"), D("bk"))
-        for c in range(4): vr(D("bst", c, c + 1), D("t1", 16 * c, 16 * c + 16), A.min)
-        vc(D("bi"), D("bst")); vt(D("t0"), D("bst"), D("i64"), A.add)
+        vscan(D("bsc"), D("s16"), D("t1"), 0.0, A.max, A.min)
+        vc(D("bi"), D("bsc", 15, 64, 16)); vt(D("t0"), D("bsc", 15, 64, 16), D("i64"), A.add)
         vs(D("jb64"), D("bi"), 4032, A.bitwise_and)
         vt(D("tt1"), D("t0"), D("jb64"), A.subtract); vt(D("okc"), D("jb64"), D("i64"), A.is_gt); vc(D("jf"), D("jb64"))
         vt(D("pk"), D("tt1"), D("okc"), A.mult)
@@ -267,28 +335,25 @@ def rank_program(g, core, T, topo):
                 vs(D("pm0", 64 * s, 64 * s + 64) if b == 0 else D("pv", 64 * s, 64 * s + 64), D("j64"), D("jf", c, c + 1), A.is_equal, D("pk", c, c + 1), A.mult)
         vt(D("px"), D("pm0"), D("pv", 0, 128), A.min)
         vx(D("t2"), D("px"))
-        for b in range(2):
-            for s in range(2):
-                vr(D("acc", 2 * b + s, 2 * b + s + 1), D("t2", 64 * s + 32 * b, 64 * s + 32 * b + 32), A.min)
-        vt(D("ai"), D("acc"), D("defn"), A.min); vs(D("got"), D("acc"), 0.0, A.is_lt)
+        vscan(D("acs"), D("s32"), D("t2"), 0.0, A.max, A.min)
+        vt(D("ai"), D("acs", 31, 128, 32), D("defn"), A.min); vs(D("got"), D("acs", 31, 128, 32), 0.0, A.is_lt)
         vs(D("pa"), D("ai"), 4032, A.bitwise_and, 6, A.logical_shift_right)
         vs(D("oh"), D("ai"), 62, A.bitwise_and, 1, A.logical_shift_right)
         vc(D("pf"), D("pa"))
-        for s in range(2):
-            for x in range(2): vt(D("pl%d" % s, x, 4, 2), D("pa", s, 4, 2), D("mm%d" % x), A.mult)
-        for c in range(4): sa(D("z", 16 * c, 16 * c + 16), D("z64", 0, 16), F.Identity, D("pf", c, c + 1))
-        pe(D("plf", 0, 4), [(D("u0"), D("pl0")), (D("u1"), D("pl1"))])
+        for x in range(2): vt(D("pl", x, 8, 2), D("pa"), D("mm%d" % x), A.mult)
+        bs = (0, 2, 1, 3)
+        for c in range(4): sa(D("z", 16 * c, 16 * c + 16), D("z64", 0, 16), F.Identity, D("pf", bs[c], bs[c] + 1))
+        pe(D("plf", 0, 4), [(D("u0"), D("pl", 0, 4)), (D("u1"), D("pl", 4, 8))])
         vt(D("cut"), D("oh"), D("got"), A.add)
         vx(D("r1"), D("z")); vc(D("l1"), D("plf", 0, 4))
         L1 = D("l1"); L4 = D("l4"); L16 = D("l16")
-        for s in range(2):
-            for x in range(2): sa(D("cl%d" % s, x, 4, 2), D("cut", s, 4, 2), F.Identity, 0.0, D("m%d" % x))
-        for c in range(4): sa(D("zc", 16 * c, 16 * c + 16), D("z64", 0, 16), F.Identity, D("cut", c, c + 1))
+        for x in range(2): sa(D("cl", x, 8, 2), D("cut"), F.Identity, 0.0, D("m%d" % x))
+        for c in range(4): sa(D("zc", 16 * c, 16 * c + 16), D("z64", 0, 16), F.Identity, D("cut", bs[c], bs[c] + 1))
         vc(D("r2"), IND(D("r1"), L1))
         vc(D("r3"), IND(D("r2"), L1))
         vt(D("rl"), IND(D("r3"), L1), D("mdg"), A.mult); vc(D("r4"), IND(D("r3"), L1))
         vscan(D("sl"), D("rst"), D("rl"), 0.0, A.mult, A.add)
-        pe(D("plf", 4, 8), [(D("u0"), D("cl0")), (D("u1"), D("cl1"))])
+        pe(D("plf", 4, 8), [(D("u0"), D("cl", 0, 4)), (D("u1"), D("cl", 4, 8))])
         vx(D("cr"), D("zc"))
         vc(L4, D("sl", 15, 64, 16))
         vs(D("lenl"), D("plf", 4, 8), -1.0, A.mult, 64.0, A.add)
@@ -320,13 +385,14 @@ def rank_program(g, core, T, topo):
         vc(IND(D("dw"), D("tl")), D("vv"))
         vs(D("sp"), D("si"), 6, A.logical_shift_right)
         vscan(D("ls"), D("c16"), D("dw"), -1000.0, A.add, A.max)
-        for a in range(2):
-            lo, hi = 128 * a, 128 * a + 128
-            vc(D("lsi", lo, hi), D("ls", lo, hi)); vs(D("lsa", lo, hi), D("lsi", lo, hi), 4095, A.bitwise_and); vc(D("lay", lo, hi), D("lsa", lo, hi))
+        hv = ((0, 128), (128, 256))
+        for lo, hi in hv: vc(D("lsi", lo, hi), D("ls", lo, hi))
+        for lo, hi in hv: vs(D("lsa", lo, hi), D("lsi", lo, hi), 4095, A.bitwise_and)
+        for lo, hi in hv: vc(D("lay", lo, hi), D("lsa", lo, hi))
         sa(D("xp", 0, 2048), IND(D(X), D("lay", 0, 128)), F.Copy)
-        sa(D("xp", 2048, 16 * LAYS), IND(D(X), D("lay", 128, LAYS)), F.Copy)
+        sa(D("xp", 2048, 16 * LAYS[t]), IND(D(X), D("lay", 128, LAYS[t])), F.Copy)
         if not last: vt(D("lp"), D("h63"), D("sp"), A.add)
-        for k in range(nq): vt(D("pp", k, 64 * nq, nq), D("qh", k, 64 * nq, nq), D("sp"), A.add)
+        for k in range(nq): vt(D("pp", k, 64 * nq, nq), D("pw", k, 64 * nq, nq), D("sp"), A.add)
         if not last:
             vs(D("lw"), D("lp"), D("lcol"), A.is_ge, D("lcol"), A.mult)
         vs(D("pv", 0, 64 * nq), D("pp", 0, 64 * nq), D("lcol"), A.is_ge, D("lcol"), A.mult)
@@ -335,9 +401,9 @@ def rank_program(g, core, T, topo):
         if not last: vt(D("lm"), D("lq"), D("mdg"), A.mult)
         vc(D("kl", 0, 64 * nq), D("pq", 0, 64 * nq))
         if not last: vscan(D("lsc"), D("rst"), D("lm"), 0.0, A.mult, A.add)
-        vc(D("xp", 16 * LAYS, 4096), IND(D(X), D("lay", LAYS, 256)))
+        vc(D("xp", 16 * LAYS[t], 4096), IND(D(X), D("lay", LAYS[t], 256)))
         if not last: vc(D("lx"), D("lsc", 15, 64, 16))
-        w = 256 * nq
+        w = width(t)
         XN = "yb" if last else ("xa" if t == 1 else "xb")
         KB = "kb%d" % t
         if not last:
@@ -366,13 +432,28 @@ def rank_program(g, core, T, topo):
                 d = T.cores[(rank + k + 1) % n_ranks]
                 rid, pid = topo.addr(d, core)
                 sync_for("g", [], D(KB, k * w, k * w + w)[1])
-                g.remote_dma(T[XN][:, rank * w:rank * w + w], T[KB][:, k * w:k * w + w], T.sem["ar%d_%d" % (t, k + 1)], T.sem["tx%d" % t], pid, rid, topo.mask(core, d))
+                ar = T.sem["ar%d_%d" % (t, k + 1)]; tx = T.sem["tx%d" % t]
+                mask = topo.mask(core, d)
+                if k in RELAY[t]:
+                    hc = helpers(core)[k]
+                    hrid, hpid = topo.addr(hc, core)
+                    he = hop_engines(core, hc, d)
+                    m = k * w + w // 2
+                    g.remote_dma_fused([
+                        RemoteDMATransfer(dst_ids=[DstId(rid=hrid, pnc=hpid)], dma_engine_mask=sum(1 << e for e in he), remote_sem=T.sem["ra%d" % t], src=T[KB][:, m:k * w + w], dst=T[KB][:, m:k * w + w]),
+                        RemoteDMATransfer(dst_ids=[DstId(rid=rid, pnc=pid)], dma_engine_mask=mask, remote_sem=ar, src=T[KB][:, k * w:m], dst=T[XN][:, rank * w:rank * w + w // 2])], local_sem=tx)
+                    sent[t] += len(he)
+                else:
+                    g.remote_dma(T[XN][:, rank * w:rank * w + w], T[KB][:, k * w:k * w + w], ar, tx, pid, rid, mask)
+                sent[t] += len(topo.engines(core, d))
         if not last:
             vc(D(XLN, 16 * rank, 16 * rank + 16), D(XK, 48, 64))
             vm(D("dw"), 0.0)
         for k in range(1, 4):
             p = (rank - k) % n_ranks
-            source("AR%d_%d" % (t, k), "ar%d_%d" % (t, k), len(topo.engines(T.cores[p], core)), D(XN, p * w, p * w + w)[1])
+            cnt = len(topo.engines(T.cores[p], core))
+            if k - 1 in RELAY[t]: cnt += len(topo.engines(helpers(T.cores[p])[k - 1], core))
+            source("AR%d_%d" % (t, k), "ar%d_%d" % (t, k), cnt, D(XN, p * w, p * w + w)[1])
 
     for k in range(4):
         p = (rank - k) % n_ranks
@@ -380,7 +461,7 @@ def rank_program(g, core, T, topo):
         g.sync.dma_start(T.y[:, p * 512:p * 512 + 512], T.yb[:, p * 512:p * 512 + 512]).then_inc(T.sem.stor, 16)
     g.sync.wait_ge(T.sem.stor, 64)
     for t in range(3):
-        g.wait_ge(T.sem["tx%d" % t], sum(len(topo.engines(core, T.cores[(rank + k) % n_ranks])) for k in (1, 2, 3)))
+        g.wait_ge(T.sem["tx%d" % t], sent[t])
         if t < 2: g.wait_ge(T.sem["ux%d" % t], 6)
     for q in ("v", "s", "t", "g"):
         wait("g", q, count[q])

@@ -5,27 +5,29 @@ NV = 38
 NS = 64 - NV
 VCH = [2, 2, 2, 1, 1]
 SCH = [7, 3, 2, NS - 12, 0]
-SGR = [8, 8, NS - 16]
+SGR = [8, 12, NS - 20]
 RELU = (3, 4)
-RELAY = ((0, 1), (0, 1), ())
-LAYS = (162, 162, 148)
+RELAY = ((512, 512, 128), (512, 512, 128), (256, 256, 0))
+LAYS = (166, 166, 152)
+LAY0 = 64
 BIG = 16777216
 SC = NV * 8
 
 _F32 = [("wtf", 1), ("kmf", 24), ("thf", 8), ("mdg", 64), ("rst", 64), ("rcol", 1), ("qcol", 4), ("qj", 4), ("iq", 4), ("i64", 4), ("ib", 4), ("idf", 4), ("df", 4), ("defn", 4),
-        ("s16", 64), ("s32", 128), ("j64", 64), ("ej", 64), ("jj", 64), ("z64", 64), ("m0", 1), ("m1", 1), ("mm0", 4), ("mm1", 4), ("c16", 256), ("kp", 64), ("th4", 512),
-        ("nx", 64), ("uk", 512), ("nk", 512), ("mk", 512), ("tm0", 2 * NV), ("tm1", NV),
-        ("ta", 4 * NS), ("tb", 2 * NS), ("bk", 64), ("t1", 64), ("bsc", 64), ("t0", 4), ("jf", 4), ("okc", 4), ("tt1", 4), ("pk", 4),
+        ("s16", 64), ("s32", 128), ("j64", 64), ("jp", 64), ("jm0", 64), ("jm1", 64), ("ej", 64), ("jj", 64), ("z64", 64), ("m0", 1), ("m1", 1), ("mm0", 4), ("mm1", 4),
+        ("c16", 256), ("kp", 64), ("th4", 512),
+        ("nx", 64), ("uf", 64), ("uk", 512), ("nk", 512), ("mk", 512), ("tm0", 2 * NV), ("tm1", NV),
+        ("ta", 4 * NS), ("tb", 2 * NS), ("bk", 64), ("t1", 64), ("bsc", 64), ("t0", 4), ("jf", 4), ("tt1", 4),
         ("pm0", 128), ("px", 128), ("t2", 128), ("acs", 128), ("got", 4), ("cut", 4), ("pf", 4), ("z", 64), ("zc", 64), ("r1", 64), ("cr", 64), ("er", 64),
         ("r2", 64), ("r3", 64), ("r4", 64), ("rl", 64), ("sl", 64), ("r8", 64), ("r12", 64), ("r16", 64), ("rl2", 64), ("sl2", 64), ("r32", 64), ("r48", 64),
-        ("kr", 66), ("rl3", 64), ("sl3", 64), ("keyl", 4), ("lenl", 4), ("pm", 64), ("ps", 64), ("mlt", 64), ("x1", 64), ("ww", 64), ("vvv", 64), ("vv", 128),
-        ("dw", 256), ("ls", 256), ("hp", 64), ("h63", 64), ("lcol", 1), ("pp", 256), ("pq", 256), ("lp", 64), ("lw", 64), ("lq", 64), ("lm", 64), ("lsc", 64)]
+        ("kr", 66), ("rl3", 64), ("sl3", 64), ("lenl", 4), ("pm", 64), ("ps", 64), ("mlt", 64), ("ww", 64), ("ew", 64), ("vvv", 64), ("vv", 128),
+        ("dw", 256), ("ls", 256), ("hf", 64), ("hp", 64), ("h63", 64), ("lcol", 1), ("pp", 256), ("pq", 256), ("lp", 64), ("lw", 64), ("lq", 64), ("lm", 64), ("lsc", 64)]
 _I32 = [("wti", 1), ("kmi", 24), ("thi", 8), ("ia", 64), ("ibb", 64), ("icc", 1), ("id4", 4), ("ixo", 2 * NV), ("iu", 128), ("ui", 64), ("um", 64), ("uu", 64), ("vi", 64),
-        ("cp", 512), ("ci", 512), ("bi", 4), ("jb64", 4), ("ai", 4), ("pa", 4), ("oh", 4), ("pi", 64), ("pr", 64), ("p32", 64), ("tl4", 4), ("lsi", 256), ("lsa", 256),
+        ("cp", 512), ("ci", 512), ("bi", 4), ("jb64", 4), ("ai", 4), ("pa", 4), ("oh", 4), ("pi", 64), ("pr", 64), ("tl4", 4), ("lsi", 256), ("lsa", 256),
         ("h31", 64), ("si", 64), ("sp", 64)]
 _BF = [("xa", 4096), ("xb", 4096), ("xl0", 64), ("xl1", 64), ("xl2", 64), ("xp", 4096), ("kb0", 3072), ("kb1", 3072), ("kb2", 1536), ("yb", 2048),
        ("xk0", 64), ("xk1", 64), ("ones", 128), ("bt", 128), ("blk", 128), ("wb", 128), ("sel", 144), ("sel2", 144), ("seln", 144), ("nb", 128),
-       ("u0", 128), ("u1", 128), ("b32", 128), ("b3t", 128), ("wm", 128), ("wm2", 128),
+       ("u0", 128), ("u1", 128), ("b32", 128), ("b3t", 128), ("wm", 128), ("wm2", 128), ("lb0", 128), ("lb1", 128), ("lb2", 128), ("lb3", 128),
        ("xr", 32 * NV), ("dv0", 32 * NV), ("dv1", 32 * NV), ("dv2", 32 * NV), ("av0", 32 * NV), ("av1", 32 * NV), ("av2", 32 * NV),
        ("rv0", 32 * NV), ("rv1", 32 * NV), ("rv2", 32 * NV), ("as", 128 * NS),
        ("pl", 8), ("cl", 8), ("cc0", 66), ("cc1", 66), ("cc2", 66), ("cc3", 66)]
@@ -67,12 +69,12 @@ def rank_program(g, core, T, topo):
             if core not in hs: continue
             k = hs.index(core)
             for t in range(3):
-                if k not in RELAY[t]: continue
+                if k >= len(RELAY[t]) or not RELAY[t][k]: continue
                 d = T.cores[(r + k + 1) % n_ranks]
                 rid, pid = topo.addr(d, core)
-                w = width(t); KB = "kb%d" % t; XN = "xa" if t == 1 else "xb" if t == 0 else "yb"
+                w = width(t); f = RELAY[t][k]; KB = "kb%d" % t; XN = "xa" if t == 1 else "xb" if t == 0 else "yb"
                 g.wait_ge(T.sem["ra%d" % t], len(hop_engines(rc, core, d)))
-                g.remote_dma(T[XN][:, r * w + w // 2:r * w + w], T[KB][:, k * w + w // 2:k * w + w], T.sem["ar%d_%d" % (t, k + 1)], T.sem["tx%d" % t], pid, rid, topo.mask(core, d))
+                g.remote_dma(T[XN][:, r * w + w - f:r * w + w], T[KB][:, k * w + w - f:k * w + w], T.sem["ar%d_%d" % (t, k + 1)], T.sem["tx%d" % t], pid, rid, topo.mask(core, d))
                 g.wait_ge(T.sem["tx%d" % t], len(topo.engines(core, d)))
         return
     queue = {"v": g.vector, "s": g.scalar, "t": g.tensor, "g": g, "y": g.sync}
@@ -150,7 +152,9 @@ def rank_program(g, core, T, topo):
 
     def vm(o, c): run("v", o, [], lambda: g.vector.memset(o[0], c))
 
-    def vscan(o, a, b, init, op0, op1): run("v", o, a[1] + b[1], lambda: g.vector.tensor_tensor_scan(o[0], a[0], b[0], init, op0, op1))
+    def vscan(o, a, b, init, op0, op1):
+        c1, k1 = col(init)
+        run("v", o, a[1] + b[1] + k1, lambda: g.vector.tensor_tensor_scan(o[0], a[0], b[0], c1, op0, op1))
 
     def vx(o, a): run("v", o, a[1], lambda: g.vector.transpose(o[0], a[0]))
 
@@ -221,37 +225,58 @@ def rank_program(g, core, T, topo):
     gsel(D("u1"), D("wm2"), [[0, 4], [1, 2], [0, 16]], A.is_gt, 0, 0)
     gi(D("kr"), [[0, 66]], 1000000, 0); gi(D("c16"), [[0, 256]], 16, 0)
     gi(D("kp", 0, 48), [[1, 3], [4, 16]], 1, 0); gi(D("kp", 48, 64), [[4, 16]], 0, 0)
+    gi(D("jp"), [[64, 64]], 64, 0)
+    for b in range(2):
+        for a in range(4):
+            o = D("jm%d" % b); q = D("jp")
+            ot, oc = PLACE["jm%d" % b][:2]; qt, qc = PLACE["jp"][:2]
+            wait("g", "g", count["g"])
+            run("g", o, q[1], lambda: g.affine_select(T[ot][32 * a:32 * a + 32, oc:oc + 64], T[qt][32 * a:32 * a + 32, qc:qc + 64], [[1, 64]], A.is_gt, 0.0, -32 * b, -1))
 
     for t in range(3):
         last = t == 2
         X = "xb" if t == 1 else "xa"
         XL = "xl%d" % t
-        if t == 0: vc(D(XL), D(X, 63, 4096, 64))
-        pe(D("pu", 0, 64), [(D("wb"), D(XL))])
-        sa(D("xr"), IND(D(XL), D("xo")), F.Copy)
-        vc(D("ui"), D("pu", 0, 64)); vs(D("um"), D("ui"), 4095, A.bitwise_and)
-        vt(D("uu"), D("um"), D("um"), A.mult); vs(D("vi"), D("uu"), 5, A.logical_shift_right)
+
+        def hashes(lo, hi):
+            pe(D("pu", lo, hi), [(D("wb"), D(XL, lo, hi))])
+            vc(D("ui", lo, hi), D("pu", lo, hi)); vs(D("um", lo, hi), D("ui", lo, hi), 4095, A.bitwise_and)
+            vt(D("uu", lo, hi), D("um", lo, hi), D("um", lo, hi), A.mult); vs(D("vi", lo, hi), D("uu", lo, hi), 5, A.logical_shift_right)
+
+        def times(o, lo, hi, m):
+            k = D("kmf", t * 8 + m, t * 8 + m + 1)
+            if t or (lo == 0 and m > 1): sa(o, D("uf", lo, hi), F.Identity, 0.0, k)
+            else: vs(o, D("um", lo, hi), k, A.mult)
 
         def lists(ms):
-            for m in ms: vs(D("uk", m * NV, m * NV + NV), D("um", 0, NV), D("kmf", t * 8 + m, t * 8 + m + 1), A.mult)
+            for m in ms: times(D("uk", m * NV, m * NV + NV), 0, NV, m)
             for m in ms: vt(D("cp", m * NV, m * NV + NV), D("uk", m * NV, m * NV + NV), D("vi", 0, NV), A.add)
             lo, hi = ms[0] * NV, ms[-1] * NV + NV
             vs(D("ci", lo, hi), D("cp", lo, hi), 4095, A.bitwise_and); vc(D("of", lo, hi), D("ci", lo, hi))
-        lists([0, 1])
-        vs(D("nx"), D(XL), -1.0, A.mult)
-        for m in range(8): vs(D("uk", SC + m, 512, 8), D("um", NV, 64), D("kmf", t * 8 + m, t * 8 + m + 1), A.mult)
-        for m in range(8): vt(D("cp", SC + m, 512, 8), D("uk", SC + m, 512, 8), D("vi", NV, 64), A.add)
-        vs(D("ci", SC, 512), D("cp", SC, 512), 4095, A.bitwise_and); vc(D("of", SC, 512), D("ci", SC, 512))
+
+        def slists():
+            sa(D("nx", NV, 64), D(XL, NV, 64), F.Copy, 0.0, -1.0)
+            for m in range(8): times(D("uk", SC + m, 512, 8), NV, 64, m)
+            for m in range(8): vt(D("cp", SC + m, 512, 8), D("uk", SC + m, 512, 8), D("vi", NV, 64), A.add)
+            vs(D("ci", SC, 512), D("cp", SC, 512), 4095, A.bitwise_and); vc(D("of", SC, 512), D("ci", SC, 512))
+        if t == 0:
+            vc(D(XL), D(X, 63, 4096, 64))
+            sa(D("xr"), IND(D(XL), D("xo")), F.Copy)
+            hashes(0, 64)
+            lists([0, 1]); vc(D("uf"), D("um")); slists()
+        else:
+            hashes(0, 64)
+            vc(D("uf"), D("um"))
+            lists(list(range(8))); slists()
+            sa(D("xr"), IND(D(XL), D("xo")), F.Copy)
         nq = 2 if last else 4
 
         def strides():
             vs(D("h31"), D("um"), 31, A.bitwise_and)
-            for k in range(4): vs(D("hp", 16 * k, 16 * k + 16), D("h31", (k + 1) % 4, 64, 4), 1.0, A.add)
-            for k in range(nq): vs(D("pw", k, 64 * nq, nq), D("hp"), D("qcol", k, k + 1), A.mult)
-            if not last: vs(D("h63"), D("hp"), 63.0, A.mult)
-        if t > 0:
-            lists(list(range(2, 8)))
-            strides()
+            vs(D("hf"), D("h31"), 1.0, A.add)
+            for k in range(4): sa(D("hp", 16 * k, 16 * k + 16), D("hf", (k + 1) % 4, 64, 4), F.Copy)
+            for k in range(nq): sa(D("pw", k, 64 * nq, nq), D("hp"), F.Identity, 0.0, D("qcol", k, k + 1))
+            if not last: sa(D("h63"), D("hp"), F.Copy, 0.0, 63.0)
         bank = ["pd0", "pd0", "pd1", "pd1", "pu"]
         at = [0, 2 * NV, 0, 2 * NV, 0]
         sbank = ["pds", "pds", "plf"]
@@ -312,14 +337,15 @@ def rank_program(g, core, T, topo):
             yield vt(D("tm0", 0, NV), M(4), M(5), A.min)
             yield vt(D("tm1"), D("tm0", 0, NV), M(6), A.min)
             yield vt(bv, bv, D("tm1"), A.min)
-        vgather(0); sgather(0)
+        vgather(0)
         if t == 0: lists(list(range(2, 8)))
+        sgather(0)
         vgather(1); vsums(0); sgather(1); ssums(0)
         vgather(2); vsums(1); sgather(2); vsums(2); sgather(3)
         posts([("pd0", 0, 0, 4 * NV)]); weave(amin())
         vgather(3); vsums(3); ssums(1)
-        if t == 0: strides()
         vgather(4); vsums(4); ssums(2)
+        strides()
         posts([("pd1", 0, 4 * NV, 3 * NV), ("pds", 0, SC, 8 * s0[2])]); weave(bmin(), smin(0), smin(1))
         posts([("pu", 0, 7 * NV, NV), ("plf", 0, SC + 8 * s0[2], 8 * SGR[2])])
         weave(smin(2), iter([vt(bv, bv, M(7), A.min)]))
@@ -327,22 +353,24 @@ def rank_program(g, core, T, topo):
         vscan(D("bsc"), D("s16"), D("t1"), 0.0, A.max, A.min)
         vc(D("bi"), D("bsc", 15, 64, 16)); vt(D("t0"), D("bsc", 15, 64, 16), D("i64"), A.add)
         vs(D("jb64"), D("bi"), 4032, A.bitwise_and)
-        vt(D("tt1"), D("t0"), D("jb64"), A.subtract); vt(D("okc"), D("jb64"), D("i64"), A.is_gt); vc(D("jf"), D("jb64"))
-        vt(D("pk"), D("tt1"), D("okc"), A.mult)
+        vt(D("tt1"), D("t0"), D("jb64"), A.subtract); vs(D("jf"), D("jb64"), 64.0, A.add)
         for b in range(2):
             for s in range(2):
                 c = 2 * b + s
-                vs(D("pm0", 64 * s, 64 * s + 64) if b == 0 else D("pv", 64 * s, 64 * s + 64), D("j64"), D("jf", c, c + 1), A.is_equal, D("pk", c, c + 1), A.mult)
+                vs(D("pm0", 64 * s, 64 * s + 64) if b == 0 else D("pv", 64 * s, 64 * s + 64), D("jm%d" % b), D("jf", c, c + 1), A.is_equal, D("tt1", c, c + 1), A.mult)
         vt(D("px"), D("pm0"), D("pv", 0, 128), A.min)
         vx(D("t2"), D("px"))
         vscan(D("acs"), D("s32"), D("t2"), 0.0, A.max, A.min)
-        vt(D("ai"), D("acs", 31, 128, 32), D("defn"), A.min); vs(D("got"), D("acs", 31, 128, 32), 0.0, A.is_lt)
+        vt(D("ai"), D("acs", 31, 128, 32), D("defn"), A.min); sa(D("got"), D("acs", 31, 128, 32), F.Sign, 0.0, -1.0)
         vs(D("pa"), D("ai"), 4032, A.bitwise_and, 6, A.logical_shift_right)
         vs(D("oh"), D("ai"), 62, A.bitwise_and, 1, A.logical_shift_right)
         vc(D("pf"), D("pa"))
         for x in range(2): vt(D("pl", x, 8, 2), D("pa"), D("mm%d" % x), A.mult)
         bs = (0, 2, 1, 3)
-        for c in range(4): sa(D("z", 16 * c, 16 * c + 16), D("z64", 0, 16), F.Identity, D("pf", bs[c], bs[c] + 1))
+        for c in range(4):
+            zo = D("z", 16 * c, 16 * c + 16); zi = D("pf", bs[c], bs[c] + 1)
+            if c < 2: sa(zo, D("z64", 0, 16), F.Identity, zi)
+            else: vs(zo, D("z64", 0, 16), zi, A.add)
         pe(D("plf", 0, 4), [(D("u0"), D("pl", 0, 4)), (D("u1"), D("pl", 4, 8))])
         vt(D("cut"), D("oh"), D("got"), A.add)
         vx(D("r1"), D("z")); vc(D("l1"), D("plf", 0, 4))
@@ -351,16 +379,17 @@ def rank_program(g, core, T, topo):
         for c in range(4): sa(D("zc", 16 * c, 16 * c + 16), D("z64", 0, 16), F.Identity, D("cut", bs[c], bs[c] + 1))
         vc(D("r2"), IND(D("r1"), L1))
         vc(D("r3"), IND(D("r2"), L1))
-        vt(D("rl"), IND(D("r3"), L1), D("mdg"), A.mult); vc(D("r4"), IND(D("r3"), L1))
+        vt(D("rl"), IND(D("r3"), L1), D("mdg"), A.mult); sa(D("r4"), IND(D("r3"), L1), F.Copy)
         vscan(D("sl"), D("rst"), D("rl"), 0.0, A.mult, A.add)
         pe(D("plf", 4, 8), [(D("u0"), D("cl", 0, 4)), (D("u1"), D("cl", 4, 8))])
         vx(D("cr"), D("zc"))
         vc(L4, D("sl", 15, 64, 16))
-        vs(D("lenl"), D("plf", 4, 8), -1.0, A.mult, 64.0, A.add)
+        sa(D("lenl"), D("plf", 4, 8), F.Copy, 64.0, -1.0)
+        for q in range(4): sa(D("lb%d" % q), D("blk"), F.Identity, 0.0, D("lenl", q, q + 1))
         vc(D("r8"), IND(D("r4"), L4))
         vt(D("er"), D("cr"), D("ej"), A.add)
         vc(D("r12"), IND(D("r8"), L4))
-        vt(D("rl2"), IND(D("r12"), L4), D("mdg"), A.mult); vc(D("r16"), IND(D("r12"), L4))
+        vt(D("rl2"), IND(D("r12"), L4), D("mdg"), A.mult); sa(D("r16"), IND(D("r12"), L4), F.Copy)
         vscan(D("sl2"), D("rst"), D("rl2"), 0.0, A.mult, A.add)
         vc(L16, D("sl2", 15, 64, 16))
         vc(D("r32"), IND(D("r16"), L16))
@@ -368,29 +397,31 @@ def rank_program(g, core, T, topo):
         vt(D("rl3"), IND(D("r48"), L16), D("mdg"), A.mult)
         vt(D("kr", 0, 64), IND(D("r48"), L16), D("jj"), A.add)
         vscan(D("sl3"), D("rst"), D("rl3"), 0.0, A.mult, A.add)
-        vt(D("keyl"), D("sl3", 15, 64, 16), D("qj"), A.add)
-        for q in range(4): vs(D("cc%d" % q, 0, 65), D("kr", 0, 65), D("keyl", q, q + 1), A.is_gt, D("lenl", q, q + 1), A.mult)
-        pe(D("ppos", 0, 65), [(D("blk"), D("cc%d" % q, 0, 65)) for q in range(4)])
+        for q in range(4): vs(D("cc%d" % q, 0, 65), D("kr", 0, 65), D("sl3", 16 * q + 15, 16 * q + 16), A.subtract, D("qj", q, q + 1), A.is_gt)
+        pe(D("ppos", 0, 65), [(D("lb%d" % q), D("cc%d" % q, 0, 65)) for q in range(4)])
+        vs(D("ww"), D("kr", 0, 64), 262144.0, A.mult); vt(D("ew"), D("er"), D("ww"), A.add)
         vt(D("pm"), D("ppos", 0, 64), D("mdg"), A.mult)
         vc(D("pi"), D("ppos", 0, 64))
         vscan(D("ps"), D("rst"), D("pm"), 0.0, A.mult, A.add)
-        vs(D("pr"), D("pi"), 15, A.bitwise_and); vs(D("p32"), D("pi"), 4064, A.bitwise_and)
+        sa(D("lcol"), D("ppos", 64, 65), F.Copy)
+        vs(D("pr"), D("pi"), 15, A.bitwise_and)
         vs(D("tl4"), D("ps", 15, 64, 16), 0.0625, A.mult, -0.46875, A.add)
-        vt(D("x1"), D("er"), D("pr"), A.subtract); vs(D("ww"), D("p32"), 128.0, A.mult)
+        vt(D("vvv"), D("ew"), D("pr"), A.subtract); vs(D("mlt"), D("pr"), D("rcol"), A.is_le)
         vc(D("tl", 0, 4), D("tl4")); vs(D("tl", 4, 8), D("tl4"), 1.0, A.add)
-        vs(D("mlt"), D("pr"), D("rcol"), A.is_le); vt(D("vvv"), D("x1"), D("ww"), A.add)
-        vc(D("lcol"), D("ppos", 64, 65))
         vt(D("vv", 0, 64), D("vvv"), D("mlt"), A.mult); vs(D("vv", 64, 128), D("vvv"), 16.0, A.add)
         vs(D("si"), D("kp"), D("lcol"), A.mult)
         vc(IND(D("dw"), D("tl")), D("vv"))
         vs(D("sp"), D("si"), 6, A.logical_shift_right)
-        vscan(D("ls"), D("c16"), D("dw"), -1000.0, A.add, A.max)
-        hv = ((0, 128), (128, 256))
-        for lo, hi in hv: vc(D("lsi", lo, hi), D("ls", lo, hi))
-        for lo, hi in hv: vs(D("lsa", lo, hi), D("lsi", lo, hi), 4095, A.bitwise_and)
-        for lo, hi in hv: vc(D("lay", lo, hi), D("lsa", lo, hi))
-        sa(D("xp", 0, 2048), IND(D(X), D("lay", 0, 128)), F.Copy)
-        sa(D("xp", 2048, 16 * LAYS[t]), IND(D(X), D("lay", 128, LAYS[t])), F.Copy)
+        vscan(D("ls", 0, LAY0), D("c16", 0, LAY0), D("dw", 0, LAY0), -1000.0, A.add, A.max)
+        vc(D("lsi", 0, LAY0), D("ls", 0, LAY0))
+        vscan(D("ls", LAY0, 256), D("c16", LAY0, 256), D("dw", LAY0, 256), D("ls", LAY0 - 1, LAY0), A.add, A.max)
+        vs(D("lsa", 0, LAY0), D("lsi", 0, LAY0), 4095, A.bitwise_and)
+        vc(D("lsi", LAY0, 256), D("ls", LAY0, 256))
+        vc(D("lay", 0, LAY0), D("lsa", 0, LAY0))
+        vs(D("lsa", LAY0, 256), D("lsi", LAY0, 256), 4095, A.bitwise_and)
+        vc(D("lay", LAY0, 256), D("lsa", LAY0, 256))
+        sa(D("xp", 0, 16 * LAY0), IND(D(X), D("lay", 0, LAY0)), F.Copy)
+        sa(D("xp", 16 * LAY0, 16 * LAYS[t]), IND(D(X), D("lay", LAY0, LAYS[t])), F.Copy)
         if not last: vt(D("lp"), D("h63"), D("sp"), A.add)
         for k in range(nq): vt(D("pp", k, 64 * nq, nq), D("pw", k, 64 * nq, nq), D("sp"), A.add)
         if not last:
@@ -426,7 +457,8 @@ def rank_program(g, core, T, topo):
             n = w // 32
             if k < 3: oa = D(KB, k * w, k * w + w // 2); ob = D(KB, k * w + w // 2, k * w + w)
             else: oa = D(XN, rank * w, rank * w + w // 2); ob = D(XN, rank * w + w // 2, rank * w + w)
-            vc(oa, IND(D("xp"), D("kl", 2 * k * n, 2 * k * n + n)))
+            if k == 3 and not last: sa(oa, IND(D("xp"), D("kl", 2 * k * n, 2 * k * n + n)), F.Copy)
+            else: vc(oa, IND(D("xp"), D("kl", 2 * k * n, 2 * k * n + n)))
             sa(ob, IND(D("xp"), D("kl", 2 * k * n + n, 2 * k * n + 2 * n)), F.Copy)
             if k < 3:
                 d = T.cores[(rank + k + 1) % n_ranks]
@@ -434,14 +466,15 @@ def rank_program(g, core, T, topo):
                 sync_for("g", [], D(KB, k * w, k * w + w)[1])
                 ar = T.sem["ar%d_%d" % (t, k + 1)]; tx = T.sem["tx%d" % t]
                 mask = topo.mask(core, d)
-                if k in RELAY[t]:
+                f = RELAY[t][k]
+                m = k * w + w - f
+                if f:
                     hc = helpers(core)[k]
                     hrid, hpid = topo.addr(hc, core)
                     he = hop_engines(core, hc, d)
-                    m = k * w + w // 2
-                    g.remote_dma_fused([
-                        RemoteDMATransfer(dst_ids=[DstId(rid=hrid, pnc=hpid)], dma_engine_mask=sum(1 << e for e in he), remote_sem=T.sem["ra%d" % t], src=T[KB][:, m:k * w + w], dst=T[KB][:, m:k * w + w]),
-                        RemoteDMATransfer(dst_ids=[DstId(rid=rid, pnc=pid)], dma_engine_mask=mask, remote_sem=ar, src=T[KB][:, k * w:m], dst=T[XN][:, rank * w:rank * w + w // 2])], local_sem=tx)
+                    hop = RemoteDMATransfer(dst_ids=[DstId(rid=hrid, pnc=hpid)], dma_engine_mask=sum(1 << e for e in he), remote_sem=T.sem["ra%d" % t], src=T[KB][:, m:k * w + w], dst=T[KB][:, m:k * w + w])
+                    on = RemoteDMATransfer(dst_ids=[DstId(rid=rid, pnc=pid)], dma_engine_mask=mask, remote_sem=ar, src=T[KB][:, k * w:m], dst=T[XN][:, rank * w:rank * w + w - f])
+                    for trs in ([[hop, on]] if 2 * f == w else [[hop], [on]]): g.remote_dma_fused(trs, local_sem=tx)
                     sent[t] += len(he)
                 else:
                     g.remote_dma(T[XN][:, rank * w:rank * w + w], T[KB][:, k * w:k * w + w], ar, tx, pid, rid, mask)
@@ -452,7 +485,7 @@ def rank_program(g, core, T, topo):
         for k in range(1, 4):
             p = (rank - k) % n_ranks
             cnt = len(topo.engines(T.cores[p], core))
-            if k - 1 in RELAY[t]: cnt += len(topo.engines(helpers(T.cores[p])[k - 1], core))
+            if RELAY[t][k - 1]: cnt += len(topo.engines(helpers(T.cores[p])[k - 1], core))
             source("AR%d_%d" % (t, k), "ar%d_%d" % (t, k), cnt, D(XN, p * w, p * w + w)[1])
 
     for k in range(4):

from concourse.bass import DstId, RemoteDMATransfer
from concourse.mybir import dt, AluOpType as A, AxisListType, ActivationFunctionType as F

NV = 38
NS = 64 - NV
VCH = [2, 2, 2, 1, 1]
SCH = [7, 3, 2, NS - 12, 0]
SGR = [8, 12, NS - 20]
RELU = (3, 4)
RELAY = ((512, 512, 128), (512, 512, 128), (256, 256, 0))
LAYS = (166, 166, 152)
LAY0 = 64
BIG = 16777216
SC = NV * 8

_F32 = [("wtf", 1), ("kmf", 24), ("thf", 8), ("mdg", 64), ("rst", 64), ("rcol", 1), ("qcol", 4), ("qj", 4), ("iq", 4), ("i64", 4), ("ib", 4), ("idf", 4), ("df", 4), ("defn", 4),
        ("s16", 64), ("s32", 128), ("j64", 64), ("jp", 64), ("jm0", 64), ("jm1", 64), ("ej", 64), ("jj", 64), ("z64", 64), ("m0", 1), ("m1", 1), ("mm0", 4), ("mm1", 4),
        ("c16", 256), ("kp", 64), ("th4", 512),
        ("nx", 64), ("uf", 64), ("uk", 512), ("nk", 512), ("mk", 512), ("tm0", 2 * NV), ("tm1", NV),
        ("ta", 4 * NS), ("tb", 2 * NS), ("bk", 64), ("t1", 64), ("bsc", 64), ("t0", 4), ("jf", 4), ("tt1", 4),
        ("pm0", 128), ("px", 128), ("t2", 128), ("acs", 128), ("got", 4), ("cut", 4), ("pf", 4), ("z", 64), ("zc", 64), ("r1", 64), ("cr", 64), ("er", 64),
        ("r2", 64), ("r3", 64), ("r4", 64), ("rl", 64), ("sl", 64), ("r8", 64), ("r12", 64), ("r16", 64), ("rl2", 64), ("sl2", 64), ("r32", 64), ("r48", 64),
        ("kr", 66), ("rl3", 64), ("sl3", 64), ("lenl", 4), ("pm", 64), ("ps", 64), ("mlt", 64), ("ww", 64), ("ew", 64), ("vvv", 64), ("vv", 128),
        ("dw", 256), ("ls", 256), ("hf", 64), ("hp", 64), ("h63", 64), ("lcol", 1), ("pp", 256), ("pq", 256), ("lp", 64), ("lw", 64), ("lq", 64), ("lm", 64), ("lsc", 64)]
_I32 = [("wti", 1), ("kmi", 24), ("thi", 8), ("ia", 64), ("ibb", 64), ("icc", 1), ("id4", 4), ("ixo", 2 * NV), ("iu", 128), ("ui", 64), ("um", 64), ("uu", 64), ("vi", 64),
        ("cp", 512), ("ci", 512), ("bi", 4), ("jb64", 4), ("ai", 4), ("pa", 4), ("oh", 4), ("pi", 64), ("pr", 64), ("tl4", 4), ("lsi", 256), ("lsa", 256),
        ("h31", 64), ("si", 64), ("sp", 64)]
_BF = [("xa", 4096), ("xb", 4096), ("xl0", 64), ("xl1", 64), ("xl2", 64), ("xp", 4096), ("kb0", 3072), ("kb1", 3072), ("kb2", 1536), ("yb", 2048),
       ("xk0", 64), ("xk1", 64), ("ones", 128), ("bt", 128), ("blk", 128), ("wb", 128), ("sel", 144), ("sel2", 144), ("seln", 144), ("nb", 128),
       ("u0", 128), ("u1", 128), ("b32", 128), ("b3t", 128), ("wm", 128), ("wm2", 128), ("lb0", 128), ("lb1", 128), ("lb2", 128), ("lb3", 128),
       ("xr", 32 * NV), ("dv0", 32 * NV), ("dv1", 32 * NV), ("dv2", 32 * NV), ("av0", 32 * NV), ("av1", 32 * NV), ("av2", 32 * NV),
       ("rv0", 32 * NV), ("rv1", 32 * NV), ("rv2", 32 * NV), ("as", 128 * NS),
       ("pl", 8), ("cl", 8), ("cc0", 66), ("cc1", 66), ("cc2", 66), ("cc3", 66)]
_U16 = [("xo", 2 * NV), ("of", 512), ("l1", 4), ("l4", 4), ("l16", 4), ("tl", 8), ("lay", 256), ("kl", 256), ("lx", 4)]
_PS = ["pu", "pd0", "pd1", "pds", "pv", "plf", "ppos", "pw"]
_OWN = ("xa", "xb", "xl0", "xl1", "xl2", "kb0", "kb1", "kb2", "yb", "xk0", "xk1", "wti", "kmi", "thi")
SCRATCH = {}
PLACE = {}
for _l, _d, _b, _al in ((_F32, "float32", "ff", 8), (_I32, "int32", "ii", 8), (_BF, "bfloat16", "bb", 16), (_U16, "uint16", "uh", 16)):
    _at = 0
    for _n, _w in _l:
        if _n in _OWN:
            SCRATCH[_n] = ("sbuf", [128, _w], _d); PLACE[_n] = (_n, 0, _w)
        else:
            PLACE[_n] = (_b, _at, _w); _at += (_w + _al - 1) // _al * _al
    SCRATCH[_b] = ("sbuf", [128, _at], _d)
for _n in _PS:
    SCRATCH[_n] = ("psum", [128, 512], "float32"); PLACE[_n] = (_n, 0, 512)
SEMAPHORES = ["sv", "ss", "st", "sg", "lx0", "lx1", "lw", "lk", "lt", "xs1", "xs2", "stor"] + ["ra%d" % t for t in range(3)]
SEMAPHORES += ["ar%d_%d" % (t, d) for t in range(3) for d in (1, 2, 3)] + ["tx%d" % t for t in range(3)] + ["ux%d" % t for t in range(2)]


def rank_program(g, core, T, topo):
    n_ranks = len(T.cores)

    def helpers(rc):
        return [c for c in topo.cores_of(rc) if topo.die(c) != topo.die(rc) and all(topo.may_write(c, d) for d in T.cores)]

    def hop_engines(rc, hc, d):
        off = topo.engines(rc, d)
        return [e for e in topo.engines(rc, hc) if e not in off]

    def width(t):
        return 512 if t == 2 else 1024
    rank = T.rank_of(core)
    if rank is None:
        for r, rc in enumerate(T.cores):
            hs = helpers(rc)
            if core not in hs: continue
            k = hs.index(core)
            for t in range(3):
                if k >= len(RELAY[t]) or not RELAY[t][k]: continue
                d = T.cores[(r + k + 1) % n_ranks]
                rid, pid = topo.addr(d, core)
                w = width(t); f = RELAY[t][k]; KB = "kb%d" % t; XN = "xa" if t == 1 else "xb" if t == 0 else "yb"
                g.wait_ge(T.sem["ra%d" % t], len(hop_engines(rc, core, d)))
                g.remote_dma(T[XN][:, r * w + w - f:r * w + w], T[KB][:, k * w + w - f:k * w + w], T.sem["ar%d_%d" % (t, k + 1)], T.sem["tx%d" % t], pid, rid, topo.mask(core, d))
                g.wait_ge(T.sem["tx%d" % t], len(topo.engines(core, d)))
        return
    queue = {"v": g.vector, "s": g.scalar, "t": g.tensor, "g": g, "y": g.sync}
    semname = {"v": "sv", "s": "ss", "t": "st", "g": "sg"}
    count = {"v": 0, "s": 0, "t": 0, "g": 0}
    value = {}
    known = {q: {} for q in queue}
    snap = {}
    sent = [0, 0, 0]
    log = {}

    def D(n, lo=0, hi=None, st=1):
        b, at, w = PLACE[n]
        if hi is None: hi = w
        hi = min(hi, w)
        return (T[b][:, at + lo:at + hi] if st == 1 else T[b][:, at + lo:at + hi:st], [(n, lo, hi, st)])

    def IND(win, off):
        return (win[0].indirect(off[0]), win[1] + off[1])

    def meet(a, b):
        if a[0] >= b[1] or b[0] >= a[1]: return False
        return not (a[2] == b[2] and a[2] > 1 and (a[0] - b[0]) % a[2] != 0)

    def sync_for(q, outs, ins):
        need = {}
        for w, keys in ((True, outs), (False, ins)):
            for (n, lo, hi, st) in keys:
                ps = SCRATCH[PLACE[n][0]][0] == "psum"
                for (src, w2, lo2, hi2, st2), k in log.get(n, {}).items():
                    hit = (ps and src != q) or ((w or w2) and meet((lo, hi, st), (lo2, hi2, st2)))
                    if hit and need.get(src, 0) < k: need[src] = k
        for src, k in need.items():
            wait(q, src, k)

    def wait(q, src, k):
        if known[q].get(src, 0) >= k: return
        queue[q].wait_ge(T.sem[semname[src]], value[(src, k)])
        for s2, k2 in list(snap[(src, k)].items()) + [(src, k)]:
            if known[q].get(s2, 0) < k2: known[q][s2] = k2

    def note(src, k, outs, ins):
        for w, keys in ((True, outs), (False, ins)):
            for (n, lo, hi, st) in keys:
                log.setdefault(n, {})[(src, w, lo, hi, st)] = k

    def done(q, ins_):
        count[q] += 1
        ins_.then_inc(T.sem[semname[q]], 1)
        value[(q, count[q])] = count[q]
        snap[(q, count[q])] = dict(known[q])
        return count[q]

    def source(name, sem, val, outs):
        semname[name] = sem
        value[(name, 1)] = val
        snap[(name, 1)] = {}
        note(name, 1, outs, [])

    def col(x):
        return (x[0], x[1]) if isinstance(x, tuple) else (x, [])

    def run(q, o, i, make):
        sync_for(q, o[1], i)
        note(q, done(q, make()), o[1], i)

    def vt(o, a, b, op): run("v", o, a[1] + b[1], lambda: g.vector.tensor_tensor(o[0], a[0], b[0], op))

    def vs(o, a, s1, op0, s2=None, op1=None):
        c1, k1 = col(s1); c2, k2 = col(s2)
        if op1 is None: run("v", o, a[1] + k1, lambda: g.vector.tensor_scalar(o[0], a[0], c1, None, op0))
        else: run("v", o, a[1] + k1 + k2, lambda: g.vector.tensor_scalar(o[0], a[0], c1, c2, op0, op1))

    def vc(o, a): run("v", o, a[1], lambda: g.vector.tensor_copy(o[0], a[0]))

    def vm(o, c): run("v", o, [], lambda: g.vector.memset(o[0], c))

    def vscan(o, a, b, init, op0, op1):
        c1, k1 = col(init)
        run("v", o, a[1] + b[1] + k1, lambda: g.vector.tensor_tensor_scan(o[0], a[0], b[0], c1, op0, op1))

    def vx(o, a): run("v", o, a[1], lambda: g.vector.transpose(o[0], a[0]))

    def sa(o, a, f, bias=0.0, scale=1.0):
        c1, k1 = col(bias); c2, k2 = col(scale)
        run("s", o, a[1] + k1 + k2, lambda: g.scalar.activation(o[0], a[0], f, bias=c1, scale=c2))

    def pe(o, *parts):
        i = []
        r = None
        for p, pairs in enumerate(parts):
            j = [k for a, b in pairs for k in a[1] + b[1]]
            sync_for("t", o[1] if p == 0 else [], j)
            i = i + j
            for n, (a, b) in enumerate(pairs):
                r = g.tensor.matmul(o[0], a[0], b[0], p == 0 and n == 0, p == len(parts) - 1 and n == len(pairs) - 1)
        note("t", done("t", r), o[1], i)

    def gi(o, pattern, base, cm):
        if SCRATCH[PLACE[o[1][0][0]][0]][2] == "int32": run("g", o, [], lambda: g.iota(o[0], pattern, base, cm))
        else: run("g", o, [], lambda: g.iota(o[0], pattern, base, cm, allow_small_or_imprecise_dtypes=True))

    def gsel(o, a, pattern, op, base, cm): run("g", o, a[1], lambda: g.affine_select(o[0], a[0], pattern, op, 0.0, base, cm))

    h = 2048
    g.sync.dma_start(T.xa[:, 0:h], T.gen0[:, 0:h]).then_inc(T.sem.lx0, 16); source("Lx0", "lx0", 16, D("xa", 0, h)[1])
    g.scalar.dma_start(T.wti[:], T.wt[:]).then_inc(T.sem.lw, 16); source("Lw", "lw", 16, D("wti")[1])
    g.scalar.dma_start(T.kmi[:], T.km[:]).then_inc(T.sem.lk, 16); source("Lk", "lk", 16, D("kmi")[1])
    g.sync.dma_start(T.xa[:, h:4096], T.gen0[:, h:4096]).then_inc(T.sem.lx1, 16); source("Lx1", "lx1", 16, D("xa", h, 4096)[1])
    g.scalar.dma_start(T.thi[:], T.th[:]).then_inc(T.sem.lt, 16); source("Lt", "lt", 16, D("thi")[1])

    vm(D("ones"), 1.0); vm(D("sel"), 0.0)
    gi(D("z64"), [[0, 64]], 0, 0)
    gsel(D("bt"), D("ones"), [[-16, 8], [0, 16]], A.is_ge, 0, 1)
    gsel(D("blk"), D("bt"), [[16, 8], [0, 16]], A.is_ge, 15, -1)
    gi(D("icc"), [[0, 1]], 0, 1); gi(D("ibb"), [[1, 64]], 0, 0); gi(D("ia"), [[1, 64]], 128, -1)
    gi(D("ixo"), [[0, 2], [1, NV]], 0, 0)
    gi(D("j64"), [[64, 64]], 0, 0); gi(D("iq"), [[16, 4]], 0, 0)
    gi(D("id4"), [[0, 4]], 0, 64); gi(D("ib"), [[2048, 2], [0, 2]], 0, 0); gi(D("idf"), [[0, 2], [2048, 2]], 0, 0)
    gi(D("iu"), [[1, 128]], 128, -1)
    gsel(D("b3t"), D("ones"), [[-32, 4], [0, 32]], A.is_ge, 0, 1)
    gsel(D("b32"), D("b3t"), [[32, 4], [0, 32]], A.is_ge, 31, -1)
    gi(D("nb"), [[0, 128]], -131072, 0)
    vc(D("wtf"), D("wti")); vc(D("kmf"), D("kmi")); vs(D("thf"), D("thi"), 4096.0, A.mult, float(-BIG), A.add)
    vs(D("sel", 15, 143, 16), D("blk", 0, 128, 16), 4096.0, A.mult)
    vs(D("wb"), D("blk"), D("wtf"), A.mult)
    vs(D("pi", 0, 1), D("icc"), 15, A.bitwise_and); vs(D("pr", 0, 1), D("icc"), 4, A.logical_shift_right, 1, A.bitwise_and)
    vc(D("rcol"), D("pi", 0, 1)); vc(D("m1"), D("pr", 0, 1))
    vs(D("um"), D("ibb"), 15, A.bitwise_and); vs(D("ui"), D("ia"), 15, A.bitwise_and)
    vs(D("rst"), D("um"), 0.0, A.not_equal); vs(D("mdg"), D("ui"), 0.0, A.is_equal)
    vc(D("xo"), D("ixo"))
    vs(D("bi"), D("id4"), 2047, A.bitwise_and); vs(D("ci", 0, 128), D("iu"), 15, A.bitwise_and)
    vt(D("i64"), D("bi"), D("ib"), A.add); vt(D("df"), D("bi"), D("idf"), A.add); vs(D("wm"), D("ci", 0, 128), 0.0, A.is_equal)
    vs(D("defn"), D("df"), -4096.0, A.add)
    vm(D("s32"), float(-2 * BIG)); vm(D("s32", 0, 128, 32), 1.0)
    vt(D("wm2"), D("wm"), D("b32"), A.mult)
    vm(D("dw"), 0.0)
    sa(D("sel2"), D("sel"), F.Copy, 0.0, 2.0); sa(D("seln"), D("sel"), F.Copy, 0.0, -1.0)
    sa(D("m0"), D("m1"), F.Copy, 1.0, -1.0)
    sa(D("mm1"), D("z64", 0, 4), F.Identity, D("m1")); sa(D("mm0"), D("z64", 0, 4), F.Identity, D("m0"))
    sa(D("s16"), D("rst"), F.Copy, 1.0, float(-2 * BIG))
    sa(D("jj"), D("j64"), F.Copy, 0.0, 1.0 / 4096); sa(D("ej"), D("j64"), F.Identity, D("rcol"))
    sa(D("qcol"), D("iq"), F.Identity, D("rcol")); sa(D("qj"), D("qcol"), F.Copy, 0.0, 0.015625)
    for m in range(8):
        sa(D("th4", m * NV, m * NV + NV), D("z64", 0, NV), F.Identity, D("thf", m, m + 1))
        sa(D("th4", SC + m, 512, 8), D("z64", 0, NS), F.Identity, D("thf", m, m + 1))
    gsel(D("u0"), D("wm2"), [[0, 4], [1, 2], [0, 16]], A.is_equal, 0, 0)
    gsel(D("u1"), D("wm2"), [[0, 4], [1, 2], [0, 16]], A.is_gt, 0, 0)
    gi(D("kr"), [[0, 66]], 1000000, 0); gi(D("c16"), [[0, 256]], 16, 0)
    gi(D("kp", 0, 48), [[1, 3], [4, 16]], 1, 0); gi(D("kp", 48, 64), [[4, 16]], 0, 0)
    gi(D("jp"), [[64, 64]], 64, 0)
    for b in range(2):
        for a in range(4):
            o = D("jm%d" % b); q = D("jp")
            ot, oc = PLACE["jm%d" % b][:2]; qt, qc = PLACE["jp"][:2]
            wait("g", "g", count["g"])
            run("g", o, q[1], lambda: g.affine_select(T[ot][32 * a:32 * a + 32, oc:oc + 64], T[qt][32 * a:32 * a + 32, qc:qc + 64], [[1, 64]], A.is_gt, 0.0, -32 * b, -1))

    for t in range(3):
        last = t == 2
        X = "xb" if t == 1 else "xa"
        XL = "xl%d" % t

        def hashes(lo, hi):
            pe(D("pu", lo, hi), [(D("wb"), D(XL, lo, hi))])
            vc(D("ui", lo, hi), D("pu", lo, hi)); vs(D("um", lo, hi), D("ui", lo, hi), 4095, A.bitwise_and)
            vt(D("uu", lo, hi), D("um", lo, hi), D("um", lo, hi), A.mult); vs(D("vi", lo, hi), D("uu", lo, hi), 5, A.logical_shift_right)

        def times(o, lo, hi, m):
            k = D("kmf", t * 8 + m, t * 8 + m + 1)
            if t or (lo == 0 and m > 1): sa(o, D("uf", lo, hi), F.Identity, 0.0, k)
            else: vs(o, D("um", lo, hi), k, A.mult)

        def lists(ms):
            for m in ms: times(D("uk", m * NV, m * NV + NV), 0, NV, m)
            for m in ms: vt(D("cp", m * NV, m * NV + NV), D("uk", m * NV, m * NV + NV), D("vi", 0, NV), A.add)
            lo, hi = ms[0] * NV, ms[-1] * NV + NV
            vs(D("ci", lo, hi), D("cp", lo, hi), 4095, A.bitwise_and); vc(D("of", lo, hi), D("ci", lo, hi))

        def slists():
            sa(D("nx", NV, 64), D(XL, NV, 64), F.Copy, 0.0, -1.0)
            for m in range(8): times(D("uk", SC + m, 512, 8), NV, 64, m)
            for m in range(8): vt(D("cp", SC + m, 512, 8), D("uk", SC + m, 512, 8), D("vi", NV, 64), A.add)
            vs(D("ci", SC, 512), D("cp", SC, 512), 4095, A.bitwise_and); vc(D("of", SC, 512), D("ci", SC, 512))
        if t == 0:
            vc(D(XL), D(X, 63, 4096, 64))
            sa(D("xr"), IND(D(XL), D("xo")), F.Copy)
            hashes(0, 64)
            lists([0, 1]); vc(D("uf"), D("um")); slists()
        else:
            hashes(0, 64)
            vc(D("uf"), D("um"))
            lists(list(range(8))); slists()
            sa(D("xr"), IND(D(XL), D("xo")), F.Copy)
        nq = 2 if last else 4

        def strides():
            vs(D("h31"), D("um"), 31, A.bitwise_and)
            vs(D("hf"), D("h31"), 1.0, A.add)
            for k in range(4): sa(D("hp", 16 * k, 16 * k + 16), D("hf", (k + 1) % 4, 64, 4), F.Copy)
            for k in range(nq): sa(D("pw", k, 64 * nq, nq), D("hp"), F.Identity, 0.0, D("qcol", k, k + 1))
            if not last: sa(D("h63"), D("hp"), F.Copy, 0.0, 63.0)
        bank = ["pd0", "pd0", "pd1", "pd1", "pu"]
        at = [0, 2 * NV, 0, 2 * NV, 0]
        sbank = ["pds", "pds", "plf"]
        scol = [0, 8 * SGR[0], 0]
        m0 = [sum(VCH[:c]) for c in range(5)]
        s0 = [sum(SGR[:c]) for c in range(4)]

        def vgather(c):
            n = 16 * VCH[c] * NV
            dv = D("dv%d" % (c % 3), 0, n)
            vt(dv, IND(D(X), D("of", m0[c] * NV, (m0[c] + VCH[c]) * NV)), D("xr", 0, n), A.subtract)
            if c in RELU: vs(D("rv%d" % (c % 3), 0, n), dv, 0.0, A.max)

        def sgather(c):
            for i in range(sum(SCH[:c]), sum(SCH[:c + 1])):
                sa(D("as", i * 128, i * 128 + 128), IND(D(X), D("of", SC + 8 * i, SC + 8 * i + 8)), F.Abs, D("nx", NV + i, NV + i + 1))
            if c not in RELU: sa(D("av%d" % (c % 3), 0, 16 * VCH[c] * NV), D("dv%d" % (c % 3), 0, 16 * VCH[c] * NV), F.Abs)

        def sums(s, b, lo, hi):
            return [(D(s, 15 - r, 143 - r), D(b, lo + r, hi, 16)) for r in range(16)]

        def vsums(c):
            n = VCH[c] * NV
            o = D(bank[c], at[c], at[c] + n)
            e = c % 3
            bias = [(D("nb"), D("ones", 0, n))]
            if c in RELU: pe(o, bias + sums("seln", "dv%d" % e, 0, 16 * n), sums("sel2", "rv%d" % e, 0, 16 * n))
            else: pe(o, bias + sums("sel", "av%d" % e, 0, 16 * n))

        def ssums(q):
            n = 8 * SGR[q]
            pe(D(sbank[q], scol[q], scol[q] + n), [(D("nb"), D("ones", 0, n))] + sums("sel", "as", s0[q] * 128, s0[q + 1] * 128))

        def posts(parts):
            for P, b, lo, n in parts: vt(D("nk", lo, lo + n), D(P, b, b + n), D("ci", lo, lo + n), A.add)
            for P, b, lo, n in parts: vt(D("pv", lo, lo + n), D(P, b, b + n), D("th4", lo, lo + n), A.is_lt)
            for P, b, lo, n in parts: vt(D("mk", lo, lo + n), D("pv", lo, lo + n), D("nk", lo, lo + n), A.mult)

        def smin(q):
            lo, hi = SC + 8 * s0[q], SC + 8 * s0[q + 1]
            a, b = s0[q], s0[q + 1]
            yield vt(D("ta", 4 * a, 4 * b), D("mk", lo, hi, 2), D("mk", lo + 1, hi, 2), A.min)
            yield vt(D("tb", 2 * a, 2 * b), D("ta", 4 * a, 4 * b, 2), D("ta", 4 * a + 1, 4 * b, 2), A.min)
            yield vt(D("bk", NV + a, NV + b), D("tb", 2 * a, 2 * b, 2), D("tb", 2 * a + 1, 2 * b, 2), A.min)

        def weave(*gs):
            for _ in range(4):
                for x in gs: next(x, None)
        bv = D("bk", 0, NV)

        def M(m, k=1): return D("mk", m * NV, (m + k) * NV)

        def amin():
            yield vt(D("tm0"), M(0, 2), M(2, 2), A.min)
            yield vt(bv, D("tm0", 0, NV), D("tm0", NV, 2 * NV), A.min)

        def bmin():
            yield vt(D("tm0", 0, NV), M(4), M(5), A.min)
            yield vt(D("tm1"), D("tm0", 0, NV), M(6), A.min)
            yield vt(bv, bv, D("tm1"), A.min)
        vgather(0)
        if t == 0: lists(list(range(2, 8)))
        sgather(0)
        vgather(1); vsums(0); sgather(1); ssums(0)
        vgather(2); vsums(1); sgather(2); vsums(2); sgather(3)
        posts([("pd0", 0, 0, 4 * NV)]); weave(amin())
        vgather(3); vsums(3); ssums(1)
        vgather(4); vsums(4); ssums(2)
        strides()
        posts([("pd1", 0, 4 * NV, 3 * NV), ("pds", 0, SC, 8 * s0[2])]); weave(bmin(), smin(0), smin(1))
        posts([("pu", 0, 7 * NV, NV), ("plf", 0, SC + 8 * s0[2], 8 * SGR[2])])
        weave(smin(2), iter([vt(bv, bv, M(7), A.min)]))
        vx(D("t1"), D("bk"))
        vscan(D("bsc"), D("s16"), D("t1"), 0.0, A.max, A.min)
        vc(D("bi"), D("bsc", 15, 64, 16)); vt(D("t0"), D("bsc", 15, 64, 16), D("i64"), A.add)
        vs(D("jb64"), D("bi"), 4032, A.bitwise_and)
        vt(D("tt1"), D("t0"), D("jb64"), A.subtract); vs(D("jf"), D("jb64"), 64.0, A.add)
        for b in range(2):
            for s in range(2):
                c = 2 * b + s
                vs(D("pm0", 64 * s, 64 * s + 64) if b == 0 else D("pv", 64 * s, 64 * s + 64), D("jm%d" % b), D("jf", c, c + 1), A.is_equal, D("tt1", c, c + 1), A.mult)
        vt(D("px"), D("pm0"), D("pv", 0, 128), A.min)
        vx(D("t2"), D("px"))
        vscan(D("acs"), D("s32"), D("t2"), 0.0, A.max, A.min)
        vt(D("ai"), D("acs", 31, 128, 32), D("defn"), A.min); sa(D("got"), D("acs", 31, 128, 32), F.Sign, 0.0, -1.0)
        vs(D("pa"), D("ai"), 4032, A.bitwise_and, 6, A.logical_shift_right)
        vs(D("oh"), D("ai"), 62, A.bitwise_and, 1, A.logical_shift_right)
        vc(D("pf"), D("pa"))
        for x in range(2): vt(D("pl", x, 8, 2), D("pa"), D("mm%d" % x), A.mult)
        bs = (0, 2, 1, 3)
        for c in range(4):
            zo = D("z", 16 * c, 16 * c + 16); zi = D("pf", bs[c], bs[c] + 1)
            if c < 2: sa(zo, D("z64", 0, 16), F.Identity, zi)
            else: vs(zo, D("z64", 0, 16), zi, A.add)
        pe(D("plf", 0, 4), [(D("u0"), D("pl", 0, 4)), (D("u1"), D("pl", 4, 8))])
        vt(D("cut"), D("oh"), D("got"), A.add)
        vx(D("r1"), D("z")); vc(D("l1"), D("plf", 0, 4))
        L1 = D("l1"); L4 = D("l4"); L16 = D("l16")
        for x in range(2): sa(D("cl", x, 8, 2), D("cut"), F.Identity, 0.0, D("m%d" % x))
        for c in range(4): sa(D("zc", 16 * c, 16 * c + 16), D("z64", 0, 16), F.Identity, D("cut", bs[c], bs[c] + 1))
        vc(D("r2"), IND(D("r1"), L1))
        vc(D("r3"), IND(D("r2"), L1))
        vt(D("rl"), IND(D("r3"), L1), D("mdg"), A.mult); sa(D("r4"), IND(D("r3"), L1), F.Copy)
        vscan(D("sl"), D("rst"), D("rl"), 0.0, A.mult, A.add)
        pe(D("plf", 4, 8), [(D("u0"), D("cl", 0, 4)), (D("u1"), D("cl", 4, 8))])
        vx(D("cr"), D("zc"))
        vc(L4, D("sl", 15, 64, 16))
        sa(D("lenl"), D("plf", 4, 8), F.Copy, 64.0, -1.0)
        for q in range(4): sa(D("lb%d" % q), D("blk"), F.Identity, 0.0, D("lenl", q, q + 1))
        vc(D("r8"), IND(D("r4"), L4))
        vt(D("er"), D("cr"), D("ej"), A.add)
        vc(D("r12"), IND(D("r8"), L4))
        vt(D("rl2"), IND(D("r12"), L4), D("mdg"), A.mult); sa(D("r16"), IND(D("r12"), L4), F.Copy)
        vscan(D("sl2"), D("rst"), D("rl2"), 0.0, A.mult, A.add)
        vc(L16, D("sl2", 15, 64, 16))
        vc(D("r32"), IND(D("r16"), L16))
        vc(D("r48"), IND(D("r32"), L16))
        vt(D("rl3"), IND(D("r48"), L16), D("mdg"), A.mult)
        vt(D("kr", 0, 64), IND(D("r48"), L16), D("jj"), A.add)
        vscan(D("sl3"), D("rst"), D("rl3"), 0.0, A.mult, A.add)
        for q in range(4): vs(D("cc%d" % q, 0, 65), D("kr", 0, 65), D("sl3", 16 * q + 15, 16 * q + 16), A.subtract, D("qj", q, q + 1), A.is_gt)
        pe(D("ppos", 0, 65), [(D("lb%d" % q), D("cc%d" % q, 0, 65)) for q in range(4)])
        vs(D("ww"), D("kr", 0, 64), 262144.0, A.mult); vt(D("ew"), D("er"), D("ww"), A.add)
        vt(D("pm"), D("ppos", 0, 64), D("mdg"), A.mult)
        vc(D("pi"), D("ppos", 0, 64))
        vscan(D("ps"), D("rst"), D("pm"), 0.0, A.mult, A.add)
        sa(D("lcol"), D("ppos", 64, 65), F.Copy)
        vs(D("pr"), D("pi"), 15, A.bitwise_and)
        vs(D("tl4"), D("ps", 15, 64, 16), 0.0625, A.mult, -0.46875, A.add)
        vt(D("vvv"), D("ew"), D("pr"), A.subtract); vs(D("mlt"), D("pr"), D("rcol"), A.is_le)
        vc(D("tl", 0, 4), D("tl4")); vs(D("tl", 4, 8), D("tl4"), 1.0, A.add)
        vt(D("vv", 0, 64), D("vvv"), D("mlt"), A.mult); vs(D("vv", 64, 128), D("vvv"), 16.0, A.add)
        vs(D("si"), D("kp"), D("lcol"), A.mult)
        vc(IND(D("dw"), D("tl")), D("vv"))
        vs(D("sp"), D("si"), 6, A.logical_shift_right)
        vscan(D("ls", 0, LAY0), D("c16", 0, LAY0), D("dw", 0, LAY0), -1000.0, A.add, A.max)
        vc(D("lsi", 0, LAY0), D("ls", 0, LAY0))
        vscan(D("ls", LAY0, 256), D("c16", LAY0, 256), D("dw", LAY0, 256), D("ls", LAY0 - 1, LAY0), A.add, A.max)
        vs(D("lsa", 0, LAY0), D("lsi", 0, LAY0), 4095, A.bitwise_and)
        vc(D("lsi", LAY0, 256), D("ls", LAY0, 256))
        vc(D("lay", 0, LAY0), D("lsa", 0, LAY0))
        vs(D("lsa", LAY0, 256), D("lsi", LAY0, 256), 4095, A.bitwise_and)
        vc(D("lay", LAY0, 256), D("lsa", LAY0, 256))
        sa(D("xp", 0, 16 * LAY0), IND(D(X), D("lay", 0, LAY0)), F.Copy)
        sa(D("xp", 16 * LAY0, 16 * LAYS[t]), IND(D(X), D("lay", LAY0, LAYS[t])), F.Copy)
        if not last: vt(D("lp"), D("h63"), D("sp"), A.add)
        for k in range(nq): vt(D("pp", k, 64 * nq, nq), D("pw", k, 64 * nq, nq), D("sp"), A.add)
        if not last:
            vs(D("lw"), D("lp"), D("lcol"), A.is_ge, D("lcol"), A.mult)
        vs(D("pv", 0, 64 * nq), D("pp", 0, 64 * nq), D("lcol"), A.is_ge, D("lcol"), A.mult)
        if not last: vt(D("lq"), D("lp"), D("lw"), A.subtract)
        vt(D("pq", 0, 64 * nq), D("pp", 0, 64 * nq), D("pv", 0, 64 * nq), A.subtract)
        if not last: vt(D("lm"), D("lq"), D("mdg"), A.mult)
        vc(D("kl", 0, 64 * nq), D("pq", 0, 64 * nq))
        if not last: vscan(D("lsc"), D("rst"), D("lm"), 0.0, A.mult, A.add)
        vc(D("xp", 16 * LAYS[t], 4096), IND(D(X), D("lay", LAYS[t], 256)))
        if not last: vc(D("lx"), D("lsc", 15, 64, 16))
        w = width(t)
        XN = "yb" if last else ("xa" if t == 1 else "xb")
        KB = "kb%d" % t
        if not last:
            XK = "xk%d" % t; XLN = "xl%d" % (t + 1)
            vc(D(XK), IND(D("xp"), D("lx")))
            sync_for("g", [], D(XK, 0, 48)[1])
            trs = []
            for k in range(3):
                d = T.cores[(rank + k + 1) % n_ranks]
                rid, pid = topo.addr(d, core)
                en = topo.engines(core, d)
                mask = (1 << en[2 * k]) + (1 << en[2 * k + 1])
                trs.append(RemoteDMATransfer(dst_ids=[DstId(rid=rid, pnc=pid)], dma_engine_mask=mask, remote_sem=T.sem["xs%d" % (t + 1)],
                                             src=T[XK][:, 16 * k:16 * k + 16], dst=T[XLN][:, 16 * rank:16 * rank + 16]))
            g.remote_dma_fused(trs, local_sem=T.sem["ux%d" % t])
            for k in range(1, 4):
                p = (rank - k) % n_ranks
                source("XS%d" % (t + 1), "xs%d" % (t + 1), 6, D(XLN, 16 * p, 16 * p + 16)[1])
        for k in range(4):
            n = w // 32
            if k < 3: oa = D(KB, k * w, k * w + w // 2); ob = D(KB, k * w + w // 2, k * w + w)
            else: oa = D(XN, rank * w, rank * w + w // 2); ob = D(XN, rank * w + w // 2, rank * w + w)
            if k == 3 and not last: sa(oa, IND(D("xp"), D("kl", 2 * k * n, 2 * k * n + n)), F.Copy)
            else: vc(oa, IND(D("xp"), D("kl", 2 * k * n, 2 * k * n + n)))
            sa(ob, IND(D("xp"), D("kl", 2 * k * n + n, 2 * k * n + 2 * n)), F.Copy)
            if k < 3:
                d = T.cores[(rank + k + 1) % n_ranks]
                rid, pid = topo.addr(d, core)
                sync_for("g", [], D(KB, k * w, k * w + w)[1])
                ar = T.sem["ar%d_%d" % (t, k + 1)]; tx = T.sem["tx%d" % t]
                mask = topo.mask(core, d)
                f = RELAY[t][k]
                m = k * w + w - f
                if f:
                    hc = helpers(core)[k]
                    hrid, hpid = topo.addr(hc, core)
                    he = hop_engines(core, hc, d)
                    hop = RemoteDMATransfer(dst_ids=[DstId(rid=hrid, pnc=hpid)], dma_engine_mask=sum(1 << e for e in he), remote_sem=T.sem["ra%d" % t], src=T[KB][:, m:k * w + w], dst=T[KB][:, m:k * w + w])
                    on = RemoteDMATransfer(dst_ids=[DstId(rid=rid, pnc=pid)], dma_engine_mask=mask, remote_sem=ar, src=T[KB][:, k * w:m], dst=T[XN][:, rank * w:rank * w + w - f])
                    for trs in ([[hop, on]] if 2 * f == w else [[hop], [on]]): g.remote_dma_fused(trs, local_sem=tx)
                    sent[t] += len(he)
                else:
                    g.remote_dma(T[XN][:, rank * w:rank * w + w], T[KB][:, k * w:k * w + w], ar, tx, pid, rid, mask)
                sent[t] += len(topo.engines(core, d))
        if not last:
            vc(D(XLN, 16 * rank, 16 * rank + 16), D(XK, 48, 64))
            vm(D("dw"), 0.0)
        for k in range(1, 4):
            p = (rank - k) % n_ranks
            cnt = len(topo.engines(T.cores[p], core))
            if RELAY[t][k - 1]: cnt += len(topo.engines(helpers(T.cores[p])[k - 1], core))
            source("AR%d_%d" % (t, k), "ar%d_%d" % (t, k), cnt, D(XN, p * w, p * w + w)[1])

    for k in range(4):
        p = (rank - k) % n_ranks
        sync_for("y", [], D("yb", p * 512, p * 512 + 512)[1])
        g.sync.dma_start(T.y[:, p * 512:p * 512 + 512], T.yb[:, p * 512:p * 512 + 512]).then_inc(T.sem.stor, 16)
    g.sync.wait_ge(T.sem.stor, 64)
    for t in range(3):
        g.wait_ge(T.sem["tx%d" % t], sent[t])
        if t < 2: g.wait_ge(T.sem["ux%d" % t], 6)
    for q in ("v", "s", "t", "g"):
        wait("g", q, count[q])
